import numpy as np, ml_dtypes
CORES = [3,7,11,15,131,135,139,143]
N = 8
BF = ml_dtypes.bfloat16
V, P, Q, RO, TS = 160, 2, 2, 3, 1024
M, B = 8 * N * V, V // P
def clip(a):
    return np.minimum(np.maximum(np.floor(a), -2 ** 20), 2 ** 20 - 1).astype(np.int64)
def walls(rng, base, size, gap):
    mid = base + size * (rng.random((N, 8, 16, V)) - 0.5)
    h = gap * (16 - np.arange(16)[:, None]) * 0.0625
    l = mid + h * rng.random((N, 8, 16, V)); r = mid - h * rng.random((N, 8, 16, V)); turn = rng.random((N, 8, 1, V)) < 0.25
    return clip(np.where(turn, r, l)), clip(np.where(turn, l, r))
def common(rng):
    return walls(rng, rng.integers(-2 ** 18, 2 ** 18, (N, 8, 1, V)), np.exp2(rng.integers(8, 18, (N, 8, 1, V))), 2.0 ** 17 * rng.random((N, 8, 1, V)))
def slots(rng):
    share = rng.choice(np.array([0.1, 0.4, 0.7, 0.9]), (N, 8, 2, 1, V))
    o = rng.integers(0, M, (N, 8, 16, V)); none = (rng.random((N, 8, 2, 8, V)) < share).reshape(N, 8, 16, V)
    return np.where(none, M, o)
def pack(l, r, o):
    return {"lw": np.ascontiguousarray(l.reshape(N, 128, V)).astype(np.int32), "rw": np.ascontiguousarray(r.reshape(N, 128, V)).astype(np.int32),
            "opts": np.ascontiguousarray(o.reshape(N, 128, V)).astype(np.int32)}
def setup_inputs(rng):
    l, r = common(rng)
    return pack(l, r, slots(rng))
def setup_inputs_ties(rng):
    ix = rng.integers(0, 5, (N, 8, V)); base = 65536 * np.array([0, 0, 12, 12, -13])[:, None] + 2 * rng.integers(-4, 5, (5, 1)); out = []
    for up in (rng.integers(0, 6), 0):
        prof = base + up + rng.integers(0, 2, (5, 16))
        a = prof[ix].transpose(0, 1, 3, 2)
        i = rng.integers(0, 16, (N, 8, 1, V)); d = rng.choice(np.array([-1, 1]), (N, 8, 1, V)) * (rng.random((N, 8, 1, V)) < 0.3)
        far = 65536 * (rng.random((N, 8, 1, V)) < 0.125)
        out.append(a + d * (np.arange(16)[:, None] == i) + far)
    return pack(out[0], out[1], np.where(rng.random((N, 8, 16, V)) < 0.3, M, rng.integers(0, M, (N, 8, 16, V))))
def setup_inputs_bare(rng):
    l, r = common(rng); kinds = np.zeros((7, 16), bool)
    kinds[1, :8] = True; kinds[2, 8:] = True; kinds[3] = True; kinds[4, [0, 15]] = True; kinds[5, [7, 8]] = True; kinds[6, 0] = True
    cls = rng.integers(0, 7, (N, 8, V)); cls[:, 3] = 0; cls[:, 5] = 3
    o = np.where(kinds[cls].transpose(0, 1, 3, 2), rng.integers(0, M, (N, 8, 16, V)), M)
    for g, s, e, d in ((1, 0, -2 ** 20, 1), (6, 15, 2 ** 20 - 1, -1)):
        l[:, g] = e + d * rng.integers(0, 64, (N, 16, V)); r[:, g] = e + d * rng.integers(0, 64, (N, 16, V))
        o[:, g] = M; o[:, g, s] = V * (8 * rng.integers(0, N, (N, V)) + g) + rng.integers(0, B, (N, V))
    return pack(l, r, o)
def setup_inputs_ends(rng):
    l, r = common(rng); o = slots(rng)
    o[:, ::2] = rng.choice(np.array([0, V - 1, V, 8 * V - 1, 8 * V, M - 1, M]), (N, 4, 16, V))
    o[:, 2] = rng.integers(0, M)
    own = V * np.arange(8 * N).reshape(N, 8, 1, 1) + np.arange(V)
    o[:, 1] = np.where(rng.random((N, 16, V)) < 0.5, own[:, 1], o[:, 1])
    o[:, 3, :8] = o[:, 3, :1]; o[:, 3, 8:] = o[:, 3, 8:9]
    here = 8 * V * np.arange(N)[:, None, None]; nxt = 8 * V * ((np.arange(N) + 1) % N)[:, None, None]
    o[:, 5] = nxt + rng.integers(0, 8 * V, (N, 16, V))
    o[:, 7] = np.where(o[:, 7] < M, here + rng.integers(0, 8 * V, (N, 16, V)), M)
    return pack(l, r, o)
def setup_inputs_late(rng):
    bump = rng.random((N, 8, 1, V)) < 0.0625; bump[:, 4] = False
    l = rng.integers(-2 ** 12, 2 ** 12, (16, 1)) + bump
    r = l + rng.choice(np.array([-3, 0, 3, 5001]), (16, 1))
    z = rng.integers(0, 8, (N, 8, 2, 1, V)); s = np.arange(8)[:, None]
    has = np.where(rng.random((N, 8, 2, 1, V)) < 0.4, s == z, s >= z).reshape(N, 8, 16, V)
    o = np.where(has, rng.integers(0, M, (N, 8, 16, V)), M)
    o[:, 4] = V * (8 * rng.integers(0, N, (N, 16, V)) + 4) + rng.integers(0, V, (N, 16, V))
    return pack(l, r, o)
def setup_inputs_spread(rng):
    base = rng.choice(np.array([-1.0, 1.0]), (N, 8, 1, V)) * np.exp2(20 * rng.random((N, 8, 1, V)))
    l, r = walls(rng, base, np.abs(base) * rng.random((N, 8, 1, V)), np.exp2(18 * rng.random((N, 8, 1, V))))
    e = rng.integers(1, 5, (1, 8, 1, 1))
    o = np.minimum((M * rng.random((N, 8, 16, V)) ** e).astype(np.int64), M - 1)
    share = rng.random((N, 8, 1, V)); share[rng.integers(0, N)] = 0.0
    return pack(l, r, np.where(rng.random((N, 8, 16, V)) < share, M, o))
def check_inputs(d):
    bad = []
    for k, lo, hi in (("lw", -2 ** 20, 2 ** 20 - 1), ("rw", -2 ** 20, 2 ** 20 - 1), ("opts", 0, M)):
        if np.min(d[k]) < lo or np.max(d[k]) > hi: bad.append("range of " + k)
    return bad
def world(a, last):
    w = a.reshape(N, 8, 16, V).transpose(2, 0, 1, 3).reshape(16, M).astype(np.int32)
    return np.concatenate([w, np.full((16, 1), last, np.int32)], axis=1)
def back(w):
    return np.ascontiguousarray(w[:, :M].reshape(16, N, 8, V).transpose(1, 2, 0, 3)).reshape(N, 128, V).astype(np.float32)
def inner(L, R, ix):
    return np.concatenate([R[:, ix[:8]], -L[:, ix[8:]]], axis=1)
def reference(lw, rw, opts):
    L, R, O = world(lw, 0), world(rw, 0), world(opts, M)
    temp = (TS * np.arange(16, dtype=np.int32))[:, None]; s16 = np.arange(16); left = (s16 < 8)[:, None]
    for t in range(RO):
        nL, nR, nO = L.copy(), R.copy(), O.copy()
        v = np.tile(B * (t % P) + np.arange(B), 8 * N); c = V * np.repeat(np.arange(8 * N), B) + v
        o = O[:, c]; xl, xr = L[:, c], R[:, c]; has = o < M
        u = inner(L, R, o); gone = np.zeros(o.shape, bool)
        for q in range(Q):
            p = s16 ^ (1 + (t + 3 * q) % 7); up = u[:, p]
            ge = np.all(up >= u, axis=0); eq = np.all(up == u, axis=0)
            gone = gone | (has & has[p] & ge & (~eq | (p < s16)[:, None]))
        sl = (v + t) & 7; k = O[np.where(left, 8 + sl, sl), o]
        kl, kr = L[:, k], R[:, k]; yl, yr = xl[:, None, :], xr[:, None, :]
        under = np.all((kl[:, :8] <= yl) & (kr[:, :8] <= yr), axis=0); over = np.all((kl[:, 8:] >= yl) & (kr[:, 8:] >= yr), axis=0)
        rev = (has & ~gone & (k < M) & np.concatenate([under, over], axis=0)).reshape(2, 8, -1).astype(np.int64)
        first = (rev == 1) & (np.add.accumulate(rev, axis=1) == 1)
        ch = np.where(np.any(first, axis=1), np.add.reduce(first * k.reshape(2, 8, -1), axis=1), M)
        ent = O[s16[:, None], np.repeat(ch, 8, axis=0)]
        n = np.where(has & ~gone & ~first.reshape(16, -1), o, ent); hn = n < M
        w = np.where(hn[None], inner(L, R, n), -2 ** 23)
        l = np.where(np.any(hn[:8], axis=0)[None], np.max(w[:, :8], axis=1) - temp, xl)
        r = np.where(np.any(hn[8:], axis=0)[None], temp - np.max(w[:, 8:], axis=1), xr)
        low = l < r; mid = (l + r) >> 1
        nL[:, c] = np.where(low, mid, l); nR[:, c] = np.where(low, mid, r); nO[:, c] = n
        L, R, O = nL, nR, nO
    return {"yl": back(L), "yr": back(R), "yo": back(O)}

@@ -1,0 +1,542 @@
+from concourse.bass import DstId, RemoteDMATransfer
+from concourse.mybir import AluOpType as A, ActivationFunctionType as AF
+
+N, V, B, E = 8, 160, 80, 10240
+BIG = 8388608.0
+MG = 12582912.0
+FI, FB, II, UU = "float32", "bfloat16", "int32", "uint16"
+SCRATCH = {
+    "W": ("sbuf", [128, E + 8], FI), "OT": ("sbuf", [128, E + 16], FB),
+    "MB": ("sbuf", [128, 1312], FB), "mI": ("sbuf", [128, 1312], II),
+    "d0": ("sbuf", [128, 160, 2, 2], FB), "d1": ("sbuf", [128, 160, 2, 2], FB),
+    "V0": ("sbuf", [128, 160, 2, 2, 2], FB), "V1": ("sbuf", [128, 160, 2, 2, 2], FB),
+    "F": ("sbuf", [128, 2304], FB), "EX": ("sbuf", [128, 80, 16], FB),
+    "t1": ("sbuf", [128, 640], FI), "t2": ("sbuf", [128, 5, 16, 2, 2], FI), "m4": ("sbuf", [128, 5, 2, 16], FI),
+    "X": ("sbuf", [128, 2, 2, 80], II), "Y": ("sbuf", [128, 2, 2, 80], FI), "TN": ("sbuf", [128, 5, 2, 16], FB),
+    "HB": ("sbuf", [128, 2, 5, 16], FB), "LB": ("sbuf", [128, 2, 5, 16], FB), "T4": ("sbuf", [128, 2, 5, 2, 16], FB),
+    "CI": ("sbuf", [128, 16], II), "CF": ("sbuf", [128, 16], FI), "CC": ("sbuf", [128, 48], FI),
+    "ci": ("sbuf", [128, 143], FI), "kr": ("sbuf", [128, 128], FI), "pr": ("sbuf", [128, 128], FI),
+    "DL": ("sbuf", [128, 16], FI), "F9": ("sbuf", [128, 9], FI),
+    "MZ": ("sbuf", [128, 720], FB), "M8": ("sbuf", [128, 1664], FB), "M4": ("sbuf", [128, 896], FI),
+}
+for _n, _w, _t in (("u w x0 x1 AW0 AW1 AW2 AW3", 1280, FI), ("gO cm1 cm2 AO0 AO1 AO2 AO3", 1280, FB), ("bI f1 f2", 256, FI),
+                   ("RAW yi si ti hI lI", 160, II), ("FT dT mT nd", 160, FB), ("LQn LQs", 160, UU),
+                   ("YO C nf tf eQ XO0 XO1 xs0 xs1 xx mm nn pp qq RF", 160, FI), ("LMn LMs L1 L2 LN slU", 80, UU), ("slT", 80, II),
+                   ("eV0 eV1 KC RS H2 kb kb2 g0 g1 gs gm gb sc da RM QF", 80, FI), ("fb cx", 10, FI), ("Mi cd cv", 10, II),
+                   ("iu cu", 10, UU)):
+    for _k in _n.split():
+        SCRATCH[_k] = ("sbuf", [128, _w], _t)
+for _k in range(8):
+    SCRATCH["P%d" % _k] = ("psum", [128, 512], FI)
+SEMAPHORES = ["qv", "qt", "qs", "qg", "ls"] + ["%s%s%d" % (a, b, e) for a in ("rw", "ro") for b in ("n", "f") for e in range(4)] \
+    + ["dm%d" % k for k in range(24)]
+
+
+def rank_program(g, core, T, topo):
+    rank = T.rank_of(core)
+    if rank is None:
+        return
+    QU = {"v": g.vector, "t": g.tensor, "s": g.scalar, "g": g, "y": g.sync}
+    tot = {}
+    waited = {q: {} for q in QU}
+    lastw, lastr = {}, {}
+    ndma = [0]
+
+    def wait(q, tok):
+        sem, val, tq = tok
+        if waited[q].get(sem, 0) < val:
+            QU[q].wait_ge(T.sem[sem], val)
+            waited[q][sem] = val
+
+    def need(q, r, w):
+        for k in r:
+            for t in lastw.get(k, []):
+                wait(q, t)
+            if k[0] == "P":
+                for t in lastr.get(k, []):
+                    if t[2] != q:
+                        wait(q, t)
+        for k in w:
+            for t in lastw.get(k, []) + lastr.get(k, []):
+                if not (q == "t" and t[2] == "t"):
+                    wait(q, t)
+
+    def done(tok, r, w):
+        for k in r:
+            lastr.setdefault(k, []).append(tok)
+        for k in w:
+            lastw[k], lastr[k] = [tok], []
+
+    def op(q, fn, r=(), w=()):
+        need(q, r, w)
+        s = "q" + q
+        tot[s] = tot.get(s, 0) + 1
+        fn(QU[q]).then_inc(T.sem[s], 1)
+        done((s, tot[s], q), r, w)
+
+    def dma(q, pairs, r=(), w=()):
+        need(q, r, w)
+        s = "dm%d" % ndma[0]
+        ndma[0] += 1
+        for o, i in pairs:
+            QU[q].dma_start(o, i).then_inc(T.sem[s], 16)
+        tot[s] = 16 * len(pairs)
+        done((s, tot[s], "d" + s), r, w)
+
+    def mm(out, pairs, r, w, first=True, last=True):
+        need("t", r, w)
+        for k, (l, x) in enumerate(pairs):
+            ins = g.tensor.matmul(out, l, x, first and k == 0, last and k == len(pairs) - 1)
+            if k == len(pairs) - 1:
+                tot["qt"] = tot.get("qt", 0) + 1
+                ins.then_inc(T.sem.qt, 1)
+                done(("qt", tot["qt"], "t"), r, w)
+
+    def ts(out, i, s1, o1, s2=None, o2=None, r=(), w=()):
+        if o2 is None:
+            op("v", lambda e: e.tensor_scalar(out, i, s1, None, o1), r, w)
+        else:
+            op("v", lambda e: e.tensor_scalar(out, i, s1, s2, o1, o2), r, w)
+
+    def tt(out, a, b, o, r, w):
+        op("v", lambda e: e.tensor_tensor(out, a, b, o), r, w)
+
+    def cp(out, i, r, w, q="v"):
+        if q == "v":
+            op("v", lambda e: e.tensor_copy(out, i), r, w)
+        else:
+            op("s", lambda e: e.activation(out, i, AF.Identity), r, w)
+
+    own = rank * 160
+    nearH = 0 if topo.host(T.cores[0]) == topo.host(core) else 1
+    partner = [c for c in T.cores if c != core and c in topo.cores_of(core)]
+    near = [c for c in T.cores if topo.host(c) == topo.host(core) and c != core and c not in partner]
+    far = [c for c in T.cores if topo.host(c) != topo.host(core)]
+    far = [c for c in far if topo.same_plane(core, c)] + [c for c in far if not topo.same_plane(core, c)]
+    offe = topo.engines(core, far[0])
+    one = [e for e in topo.engines(core, partner[0]) if e not in offe]
+    moff, mon = sum(1 << e for e in offe), sum(1 << e for e in one)
+
+    def send(kind, e):
+        name = "A%s%d" % (kind.upper(), e)
+        src = T[name][:, own:own + 160]
+        need("g", [name + "o"], [])
+
+        def tr(dst, m, sem):
+            ids = []
+            for c in dst:
+                rid, pid = topo.addr(c, core)
+                ids.append(DstId(rid=rid, pnc=pid))
+            return RemoteDMATransfer(dst_ids=ids, dma_engine_mask=m, remote_sem=T.sem[sem], srcs=[src],
+                                     dsts=[src for _ in dst], alu_op=0)
+        g.remote_dma_fused([tr(partner, mon, "r%sn%d" % (kind, e)), tr(near, moff, "r%sn%d" % (kind, e))], local_sem=T.sem.ls)
+        g.remote_dma_fused([tr(far, moff, "r%sf%d" % (kind, e))], local_sem=T.sem.ls)
+        tot["ls"] = tot.get("ls", 0) + len(one) + 2 * len(offe)
+        for s, n in (("n", len(one) + len(near) * len(offe)), ("f", len(far) * len(offe))):
+            sem = "r%s%s%d" % (kind, s, e)
+            tot[sem] = n
+            lastw[name + s] = [(sem, n, "x")]
+
+    for q, sd, t, k in (("y", 0, T.lw, "XA"), ("s", 1, T.rw, "XB")):
+        dma(q, [(T.X[64 * sd + G:64 * sd + 64:4, :, h, :], t[16 * (2 * G + h):16 * (2 * G + h) + 16, :])
+                for G in range(4) for h in range(2)], [], [k])
+    dma("y", [(T.RAW[:], T.opts[:])], [], ["RAW"])
+
+    def iota(name, pat, base=0, ch=0):
+        if name in ("CI", "mI", "slT"):
+            out = T.CI[:, 0:1] if name == "CI" else T[name][:]
+            op("g", lambda e: e.iota(out, pat, base, ch), [], [name])
+        else:
+            op("g", lambda e: e.iota(T[name][:], pat, base, ch, allow_small_or_imprecise_dtypes=True), [], [name])
+    iota("CI", [[0, 1]], 0, 1)
+    iota("ci", [[1, 143]])
+    iota("kr", [[16, 2], [0, 4], [1, 16]])
+    names = ["p", "i", "i8", "pg", "sd", "Gp", "xi", "xG", "rs", "g1", "gG", "b0", "b1", "b2"]
+    spec = [None, (0, 15), (0, 7), (4, 7), (6, 1), (4, 3), (2, 15), (0, 3), (3, 1), (4, 1), (5, 3), (0, 1), (1, 1), (2, 1)]
+    for k, s in enumerate(spec):
+        if s:
+            ts(T.CI[:, k:k + 1], T.CI[:, 0:1], s[0], A.logical_shift_right, s[1], A.bitwise_and, ["CI"], ["CI%d" % k])
+    cp(T.CF[:, 0:14], T.CI[:, 0:14], ["CI"] + ["CI%d" % k for k in range(1, 14)], ["CF"])
+    col = {n: T.CF[:, k:k + 1] for k, n in enumerate(names)}
+    ckey = {n: "CF" for n in names}
+    nc = [0]
+
+    def mk(name, src, s1, o1, s2=None, o2=None):
+        def val(s):
+            return col[s] if isinstance(s, str) else s
+        k = nc[0]
+        nc[0] += 1
+        rk = [ckey[src]] + [ckey[s] for s in (s1, s2) if isinstance(s, str)]
+        ts(T.CC[:, k:k + 1], col[src], val(s1), o1, val(s2), o2, rk, ["CC%d" % k])
+        col[name], ckey[name] = T.CC[:, k:k + 1], "CC%d" % k
+    mk("sgn", "sd", 2.0, A.mult, -1.0, A.add)
+    for b in range(2):
+        aw = T["AW%d" % b]
+        for c in range(5):
+            ts(aw[:, own + c * 32:own + c * 32 + 32], T.X[:, b, :, c::5], col["sgn"], A.mult, None, None,
+               ["XA", "XB", ckey["sgn"]], ["AW%do" % b])
+        send("w", b)
+    iota("mI", [[1, 82], [0, 16]])
+    iota("slT", [[16, 10], [0, 8]])
+    iota("RS", [[0, 10], [1, 8]])
+    iota("bI", [[1, 256]])
+    iota("KC", [[0, 10], [-16384, 8]], 141312)
+    iota("pr", [[1, 8], [0, 16]])
+    cp(T.nf[:], T.RAW[:], ["RAW"], ["nf"])
+    ts(T.tf[:], T.nf[:], 0.2, A.mult, -0.4, A.add, ["nf"], ["tf"])
+    cp(T.yi[:], T.tf[:], ["tf"], ["yi"])
+    ts(T.C[:], T.nf[:], 10240.0, A.is_ge, 5120.0, A.mult, ["nf"], ["C"])
+
+    def addterm(acc, x, f, sh, xi, si, tf, kacc, kx):
+        if sh:
+            ts(si, xi, sh, A.logical_shift_right, None, None, [kx], ["si"])
+            ts(tf, si, float(f), A.mult, None, None, ["si"], ["tf"])
+        else:
+            ts(tf, x, float(f), A.mult, None, None, [kx], ["tf"])
+        tt(acc, acc, tf, A.add, [kacc, "tf"], [kacc])
+    addterm(T.C[:], T.nf[:], 32, 0, None, None, T.tf[:], "C", "nf")
+    addterm(T.C[:], T.yi[:], -159, 0, None, None, T.tf[:], "C", "yi")
+    for sh, f in ((4, 5104), (5, -10224), (6, 608), (8, -2400), (10, 1920)):
+        addterm(T.C[:], None, f, sh, T.yi[:], T.si[:], T.tf[:], "C", "yi")
+    cp(T.ti[:], T.C[:], ["C"], ["ti"])
+    ts(T.hI[:], T.ti[:], 7, A.logical_shift_right, None, None, ["ti"], ["hI"])
+    ts(T.lI[:], T.ti[:], 127, A.bitwise_and, None, None, ["ti"], ["lI"])
+    for c in range(5):
+        cp(T.HB[:, :, c, :], T.hI[:, c::5], ["hI"], ["HB%d" % c])
+        cp(T.LB[:, :, c, :], T.lI[:, c::5], ["lI"], ["LB%d" % c])
+    mk("lo", "i", 8.0, A.is_ge)
+    mk("w", "lo", -127.0, A.mult, 128.0, A.add)
+    mk("wn", "lo", -1.0, A.mult, 1.0, A.add)
+    mk("hbw", "wn", -BIG, A.mult)
+    mk("e80", "wn", 80.0, A.mult)
+    mk("sw", "sd", -128.0, A.mult, 64.0, A.add)
+    mk("swr", "rs", -128.0, A.mult, 64.0, A.add)
+    mk("tz", "pg", 16.0, A.mult, 15.0, A.add)
+    mk("tzs", "tz", "sw", A.add)
+    mk("tl0", "pg", 16.0, A.mult, "i8", A.add)
+    mk("tl1", "tl0", 8.0, A.add)
+    mk("tl0s", "tl0", "sw", A.add)
+    mk("tl1s", "tl1", "sw", A.add)
+    mk("a1", "i", 4.0, A.mult, "pg", A.add)
+    mk("tp", "sd", 60.0, A.mult, "a1", A.add)
+    mk("tps", "tp", "sw", A.add)
+    mk("a2", "xG", 16.0, A.mult, "xi", A.add)
+    mk("xst", "sd", 64.0, A.mult, "a2", A.add)
+    mk("xot", "xst", "sw", A.add)
+    mk("a3", "pg", 8.0, A.mult, "i8", A.add)
+    mk("qt", "rs", 64.0, A.mult, "a3", A.add)
+    mk("qst", "qt", "swr", A.add)
+    mk("a4", "gG", 16.0, A.mult, "i8", A.add)
+    mk("th", "rs", 64.0, A.mult, "a4", A.add)
+    mk("tlo", "th", 8.0, A.add)
+    mk("m0", "g1", -1.0, A.mult, 1.0, A.add)
+    mk("kc", "sd", 16.0, A.mult, "i", A.add)
+    for k in range(4):
+        mk("mG%d" % k, "Gp", float(k), A.is_equal)
+    mk("tm", "i", 1024.0, A.mult)
+    mk("a5", "sd", -0.5, A.mult, 0.25, A.add)
+    mk("tb", "tm", "a5", A.add)
+    mk("a6", "b1", 3.0, A.mult, 1.0, A.add)
+    mk("a7", "b2", 15.0, A.mult, 1.0, A.add)
+    mk("a8", "b0", 1.0 / 128, A.mult, 1.0 / 128, A.add)
+    mk("a9", "a8", "a6", A.mult)
+    mk("c1", "a9", "a7", A.mult)
+    mk("s8", "i8", -1.0, A.mult, 8.0, A.add)
+
+    mats = {}
+
+    def mat(name, buf, k, width, step, row, rk, t, wgt):
+        ap = T[buf][:, k * step:k * step + width]
+        rks = [rk, ckey[t]] + ([ckey[wgt]] if isinstance(wgt, str) else [])
+        ts(ap, row, col[t], A.is_equal, col[wgt] if isinstance(wgt, str) else wgt, A.mult, rks, ["M" + name])
+        mats[name] = (buf, k * step)
+
+    def lz(name, a):
+        buf, k = mats[name]
+        return T[buf][:, k + 15 - a:k + 143 - a]
+
+    def lm(name):
+        buf, k = mats[name]
+        return T[buf][:, k:k + 128]
+    c128 = T.ci[:, 0:128]
+    for k, (n, t, m) in enumerate((("TH0", "th", "m0"), ("TL0", "tlo", "m0"), ("TH1", "th", "g1"), ("TL1", "tlo", "g1"))):
+        mat(n, "M8", k, 128, 128, c128, "ci", t, m)
+    hb = ["HB%d" % c for c in range(5)] + ["LB%d" % c for c in range(5)]
+    for b in range(2):
+        for h in range(2):
+            o = (b * 2 + h) * 80
+            mm(T.P6[:, o:o + 80], [(lm("TH%d" % h), T.HB[:, b, :, :]), (lm("TL%d" % h), T.LB[:, b, :, :])],
+               ["MTH%d" % h, "MTL%d" % h] + hb, ["P6"])
+    for b in range(2):
+        for h in range(2):
+            o = (b * 2 + h) * 80
+            cp(T.T4[:, b, :, h, :], T.P6[:, o:o + 80], ["P6"], ["T4%d%d" % (b, h)])
+        cp(T["AO%d" % b][:, own:own + 160], T.T4[:, b, :, :, :], ["T4%d0" % b, "T4%d1" % b], ["AO%do" % b])
+        send("o", b)
+    mat("QN", "M4", 0, 128, 128, c128, "ci", "qt", 1.0)
+    mat("QS", "M4", 1, 128, 128, c128, "ci", "qst", 1.0)
+    mm(T.P5[:, 0:160], [(lm("QN"), T.C[:])], ["MQN", "C"], ["P5"])
+    mm(T.P5[:, 160:320], [(lm("QS"), T.C[:])], ["MQS", "C"], ["P5"])
+    cp(T.LQn[:], T.P5[:, 0:160], ["P5"], ["LQn"])
+    cp(T.LQs[:], T.P5[:, 160:320], ["P5"], ["LQs"])
+    ts(T.eQ[:], T.P5[:, 0:160], 10240.0, A.is_ge, None, None, ["P5"], ["eQ"])
+    op("v", lambda e: e.memset(T.W[:, E:E + 8], -BIG), [], ["We"])
+    op("v", lambda e: e.memset(T.OT[:, E:E + 16], 0.0), [], ["OTz"])
+    cp(T.OT[:, E:E + 1], col["e80"], [ckey["e80"], "OTz"], ["OTe"])
+    for k in range(4):
+        mat("RG%d" % k, "M8", 4 + k, 128, 128, T.kr[:], "kr", "kc", "mG%d" % k)
+    ts(T.slU[:], T.slT[:], col["i"], A.add, None, None, ["slT", "CF"], ["slU"])
+    mat("XO", "M4", 2, 128, 128, c128, "ci", "xot", 1.0)
+    mat("XS", "M4", 3, 128, 128, c128, "ci", "xst", -1.0)
+
+    def own_walls(b, src, ksrc):
+        mm(T.P7[:, 0:160], [(lm("XO"), src)], ["MXO", ksrc], ["P7"])
+        mm(T.P7[:, 160:320], [(lm("XS"), src)], ["MXS", ksrc], ["P7"])
+        cp(T["XO%d" % b][:], T.P7[:, 0:160], ["P7"], ["XO%d" % b])
+        ts(T["xs%d" % b][:], T.P7[:, 160:320], col["tm"], A.add, None, None, ["P7", ckey["tm"]], ["xs%d" % b])
+        cp(T["x%d" % b][:], T["XO%d" % b][:].indirect(T.slU[:]), ["XO%d" % b, "slU"], ["x%d" % b], "s")
+    own_walls(0, T.AW0[:, own:own + 160], "AW0o")
+    zk = (("ZKs", "tzs", "w"), ("ZK", "tz", "w"), ("Z1", "tz", 1.0), ("ZV", "tz", -262144.0), ("ZVs", "tzs", -262144.0))
+    for k, (n, t, m) in enumerate(zk):
+        mat(n, "MZ", k, 143, 144, T.ci[:], "ci", t, m)
+    ts(T.DL[:], T.ci[:, 0:16], col["i"], A.is_equal, None, None, ["ci", "CF"], ["DL"])
+    ts(T.mI[:], T.mI[:], 7, A.bitwise_and, None, None, ["mI"], ["mI"])
+    ts(T.MB[:], T.mI[:], col["i8"], A.is_equal, None, None, ["mI", "CF"], ["MB"])
+    ts(T.RS[:], T.RS[:], 0.5, A.is_gt, None, None, ["RS"], ["RS"])
+    ts(T.H2[:], T.RS[:], 2.0, A.mult, None, None, ["RS"], ["H2"])
+
+    def empties(b, eq, keq):
+        for k in range(16):
+            op("s", lambda e: e.activation(T.EX[:, :, k], eq, AF.Identity, scale=T.DL[:, k:k + 1]), [keq, "DL"], ["EX%d" % k])
+        mm(T.P4[:, 0:80], [(lz("Z1", a), T.EX[:, 5 * a:5 * a + 5, :]) for a in range(16)],
+           ["MZ1"] + ["EX%d" % k for k in range(16)], ["P4"])
+        cp(T["eV%d" % b][:], T.P4[:, 0:80], ["P4"], ["eV%d" % b])
+    for dst, sc in (("f1", 1.0), ("f2", 0.5)):
+        ts(T[dst][:], T.bI[:], col["c1"], A.mult, sc, A.mult, ["bI", ckey["c1"]], [dst])
+        ts(T[dst][:], T[dst][:], -0.5 + 2.0 ** -9, A.add, None, None, [dst], [dst])
+        ts(T[dst][:], T[dst][:], MG, A.add, MG, A.subtract, [dst], [dst])
+    ts(T.f2[:], T.f2[:], -2.0, A.mult, None, None, ["f2"], ["f2"])
+    tt(T.f1[:], T.f1[:], T.f2[:], A.add, ["f1", "f2"], ["f1"])
+    ts(T.F9[:], T.ci[:, 0:9], col["s8"], A.is_equal, None, None, ["ci", ckey["s8"]], ["F9"])
+    for k in range(9):
+        ts(T.F[:, k::9], T.f1[:], T.F9[:, k:k + 1], A.max, None, None, ["f1", "F9"], ["F%d" % k])
+    kF = ["F%d" % k for k in range(9)]
+    for k, (n, t, m) in enumerate((("LQ0", "tl0", "w"), ("LQ1", "tl1", "w"), ("LQ0s", "tl0s", "w"), ("LQ1s", "tl1s", "w"))):
+        mat(n, "M8", 8 + k, 128, 128, c128, "ci", t, m)
+    mat("HA", "M8", 12, 128, 128, T.pr[:], "pr", "pg", "hbw")
+    mat("P1", "M4", 4, 128, 128, c128, "ci", "tp", 1.0)
+    mat("P2", "M4", 5, 128, 128, c128, "ci", "tp", 0.5)
+    mat("P3", "M4", 6, 128, 128, c128, "ci", "tps", -0.5)
+    tt(lm("P2"), lm("P2"), lm("P3"), A.add, ["MP2", "MP3"], ["MP2"])
+
+    turn = [0]
+
+    def replicate(e):
+        b = e % 2
+        aw, ao = T["AW%d" % e], T["AO%d" % e]
+        for H in (nearH, 1 - nearH):
+            kw = ["AW%do" % e, "AW%dn" % e] if H == nearH else ["AW%df" % e]
+            ko = ["AO%do" % e, "AO%dn" % e] if H == nearH else ["AO%df" % e]
+            c0 = b * 5120 + H * 2560
+            dma("y", [(T.W[16 * q:16 * q + 16, c0:c0 + 2560], aw[(64 if q < 4 else 0):(128 if q < 4 else 64), H * 640:H * 640 + 640])
+                      for q in range(8)], kw, ["W%d%d" % (b, H)])
+            for G in range(4):
+                for k in range(2):
+                    pk = "P%d" % (turn[0] % 4)
+                    o = c0 + G * 640 + k * 320
+                    mm(T[pk][:, 0:320], [(lm("RG%d" % G), ao[:, H * 640 + k * 320:H * 640 + k * 320 + 320])],
+                       ["MRG%d" % G] + ko, [pk])
+                    cp(T.OT[:, o:o + 320], T[pk][:, 0:320], [pk], ["OT%d" % o], "v" if turn[0] % 2 else "s")
+                    turn[0] += 1
+    kW = ["We"] + ["W%d%d" % (b, H) for b in range(2) for H in range(2)]
+    kOT = ["OTe"] + ["OT%d" % (320 * k) for k in range(32)]
+    W, OT = T.W[:, 0:E + 8], T.OT[:, 0:E + 16]
+
+    def invert(b):
+        f, i, s, t = T.nf[:, 0:80], T.ti[:, 0:80], T.si[:, 0:80], T.tf[:, 0:80]
+        acc, y = T.C[:, 0:80], T.yi[:, 0:80]
+        cp(i, T.QF[:], ["QF"], ["ti"])
+        ts(acc, T.QF[:], 10240.0, A.is_ge, 10080.0, A.mult, ["QF"], ["C"])
+        addterm(acc, T.QF[:], 5, 0, None, None, t, "C", "QF")
+        addterm(acc, None, 80, 4, i, s, t, "C", "ti")
+        addterm(acc, None, -319, 5, i, s, t, "C", "ti")
+        ts(s, i, 5, A.logical_shift_right, None, None, ["ti"], ["si"])
+        ts(f, s, 0.2, A.mult, -0.4, A.add, ["si"], ["nf"])
+        cp(y, f, ["nf"], ["yi"])
+        addterm(acc, y, 1275, 0, None, None, t, "C", "yi")
+        for sh, k in ((2, -4800), (4, 3840), (5, -10160)):
+            addterm(acc, None, k, sh, y, s, t, "C", "yi")
+        for c in range(5):
+            cp(T.YO[:, b * 80 + c:b * 80 + 80:5], T.C[:, c * 16:c * 16 + 16], ["C"], ["YO%d" % b])
+
+    def put_slots(b):
+        dma("y", [(T.yo[16 * gg + 8 * sd:16 * gg + 8 * sd + 8, b * 80:b * 80 + 80],
+                   T.YO[64 * sd + 8 * gg:64 * sd + 8 * gg + 8, b * 80:b * 80 + 80]) for sd in range(2) for gg in range(8)],
+            ["YO%d" % b], [])
+
+    def turn_walls(b, src, ks):
+        for c in range(5):
+            ts(T.Y[:, b, :, c::5], src[:, c * 32:c * 32 + 32], col["sgn"], A.mult, None, None, [ks, ckey["sgn"]], ["Y%d" % b])
+
+    def put_walls(b, qs):
+        for sd, o in ((0, T.yl), (1, T.yr)):
+            dma(qs[sd], [(o[16 * (2 * G + h):16 * (2 * G + h) + 16, b * 80:b * 80 + 80], T.Y[64 * sd + G:64 * sd + 64:4, b, h, :])
+                         for G in range(4) for h in range(2)], ["Y%d" % b], [])
+
+    def rnd(t):
+        b = t % 2
+        e = t + 2
+        lqn = (T.LQn[:, b * 80:b * 80 + 80], T.LQs[:, b * 80:b * 80 + 80]) if t < 2 else (T.LMn[:], T.LMs[:])
+        kl = ("LQn", "LQs") if t < 2 else ("LMn", "LMs")
+        x, kx = T["x%d" % b][:], "x%d" % b
+        op("s", lambda q: q.activation(T.u[:], W.indirect(lqn[0]), AF.Identity), kW + [kl[0]], ["u"])
+        op("v", lambda q: q.tensor_tensor(T.gO[:], OT.indirect(lqn[1]), T.MB[:, 16 * t:16 * t + 1280], A.mult), kOT + [kl[1], "MB"], ["gO"])
+        mm(T.P0[:, 0:80], [(lz("ZKs", a), T.gO[:, 80 * a:80 * a + 80]) for a in range(16)], ["MZKs", "gO"], ["P0"])
+        mm(T.P1[:, 0:80], [(lz("ZK", a), T.gO[:, 80 * a:80 * a + 80]) for a in range(16)], ["MZK", "gO"], ["P1"])
+
+        ms = [1 + (t + 3 * q) % 7 for q in range(2)]
+
+        def diffs(q):
+            m, d = ms[q], T["d%d" % q]
+            hb = m.bit_length() - 1
+            need("v", ["u"], ["d%d" % q])
+            for k in range(1 << hb):
+                out = d[:] if hb == 0 else d[:, :, :, k] if hb == 1 else d[:, :, k >> 1, k & 1]
+                tt(out, T.u[:, (k ^ m)::2 << hb], T.u[:, k::2 << hb], A.subtract, ["u"], ["d%d_%d" % (q, k)])
+            done(("qv", tot["qv"], "v"), [], ["d%d" % q])
+
+        def parts(q):
+            m, d, vv = ms[q], T["d%d" % q], T["V%d" % q]
+            hb = m.bit_length() - 1
+            f = m ^ (1 << hb)
+            need("s", ["d%d" % q], ["V%d" % q])
+
+            def act(o, i, s):
+                op("s", lambda qq: qq.activation(o, i, AF.Relu, scale=s), ["d%d" % q], [])
+            if hb == 0:
+                act(vv[:, :, :, :, 0], d[:], -1.0)
+                act(vv[:, :, :, :, 1], d[:], 1.0)
+            elif hb == 1:
+                act(vv[:, :, :, 0, :], d[:], -1.0)
+                if f == 0:
+                    act(vv[:, :, :, 1, :], d[:], 1.0)
+                else:
+                    for k in range(2):
+                        act(vv[:, :, :, 1, 1 - k], d[:, :, :, k], 1.0)
+            else:
+                act(vv[:, :, 0, :, :], d[:], -1.0)
+                if f == 0:
+                    act(vv[:, :, 1, :, :], d[:], 1.0)
+                for k in range(2 if f else 0):
+                    if f == 1:
+                        act(vv[:, :, 1, :, 1 - k], d[:, :, :, k], 1.0)
+                    else:
+                        act(vv[:, :, 1, 1 - k, :], d[:, :, k, :], 1.0)
+            done(("qs", tot["qs"], "s"), [], ["V%d" % q])
+
+        def sums(q):
+            mm(T["P%d" % (2 + q)][:, 0:80], [(lz("Z1", a), T["V%d" % q][:, 10 * a:10 * a + 10, :, :, :]) for a in range(16)],
+               ["MZ1", "V%d" % q], ["P%d" % (2 + q)])
+
+        def gone(q):
+            m, gt, gk = ms[q], T["g%d" % q], "g%d" % q
+            hb = m.bit_length() - 1
+            ts(gt[:], T["P%d" % (2 + q)][:, 0:80], 0.5, A.is_lt, None, None, ["P%d" % (2 + q)], [gk])
+            need("v", [gk], [])
+            for k in range(1 << hb):
+                op("v", lambda qq: qq.tensor_tensor(gt[:, k::2 << hb], gt[:, k::2 << hb], gt[:, (k ^ m)::2 << hb], A.is_gt))
+            done(("qv", tot["qv"], "v"), [], [gk])
+        diffs(0)
+        parts(0)
+        cp(T.L1[:], T.P0[:, 0:80], ["P0"], ["L1"])
+        op("v", lambda q: q.tensor_tensor(T.cm1[:], W.indirect(T.L1[:]), x, A.is_gt), kW + ["L1", kx], ["cm1"])
+        sums(0)
+        mm(T.P4[:, 0:80], [(lz("ZV", a), T.cm1[:, a::16]) for a in range(16)], ["MZV", "cm1"], ["P4"], True, False)
+        cp(T.L2[:], T.P1[:, 0:80], ["P1"], ["L2"])
+        diffs(1)
+        parts(1)
+        op("v", lambda q: q.tensor_tensor(T.cm2[:], W.indirect(T.L2[:]), x, A.is_lt), kW + ["L2", kx], ["cm2"])
+        sums(1)
+        mm(T.P4[:, 0:80], [(lz("ZVs", a), T.cm2[:, a::16]) for a in range(16)], ["MZVs", "cm2"], ["P4"], False, True)
+        tt(T.kb[:], T.KC[:], T.P0[:, 0:80], A.subtract, ["KC", "P0"], ["kb"])
+        gone(0)
+        gone(1)
+        tt(T.gs[:], T.g0[:], T.g1[:], A.max, ["g0", "g1"], ["gs"])
+        ts(T.gm[:], T.gs[:], -262144.0, A.mult, None, None, ["gs"], ["gm"])
+        tt(T.gb[:], T.gs[:], T["eV%d" % b][:], A.max, ["gs", "eV%d" % b], ["gb"])
+        tt(T.kb2[:], T.kb[:], T.gm[:], A.add, ["kb", "gm"], ["kb2"])
+        op("v", lambda q: q.tensor_tensor_scan(T.sc[:], T.H2[:], T.gb[:], 0.0, A.mult, A.add), ["H2", "gb"], ["sc"])
+        ts(T.fb[:], T.sc[:, 7::8], 9.0, A.mult, None, None, ["sc"], ["fb"])
+        tt(T.da[:], T.P4[:, 0:80], T.kb2[:], A.add, ["P4", "kb2"], ["da"])
+        op("v", lambda q: q.tensor_tensor_scan(T.RM[:], T.RS[:], T.da[:], 0.0, A.mult, A.max), ["RS", "da"], ["RM"])
+        cp(T.Mi[:], T.RM[:, 7::8], ["RM"], ["Mi"])
+        ts(T.cd[:], T.Mi[:], 14, A.logical_shift_right, None, None, ["Mi"], ["cd"])
+        ts(T.cv[:], T.Mi[:], 16383, A.bitwise_and, None, None, ["Mi"], ["cv"])
+        tt(T.cx[:], T.cd[:], T.fb[:], A.add, ["cd", "fb"], ["cx"])
+        ts(T.cu[:], T.cv[:], -1.0, A.mult, 10240.0, A.add, ["cv"], ["cu"])
+        cp(T.iu[:], T.cx[:], ["cx"], ["iu"])
+        op("s", lambda q: q.activation(T.FT[:], T.F[:].indirect(T.iu[:]), AF.Identity), kF + ["iu"], ["FT"])
+        old, ko = T["AO%d" % t][:, own:own + 160], "AO%do" % t
+        op("v", lambda q: q.tensor_tensor(T.dT[:], OT.indirect(T.cu[:]), old, A.subtract), kOT + ["cu", ko], ["dT"])
+        tt(T.mT[:], T.dT[:], T.FT[:], A.mult, ["dT", "FT"], ["mT"])
+        tt(T.TN[:], T.mT[:], old, A.add, ["mT", ko], ["TN"])
+        mm(T.P5[:, 0:80], [(lm("LQ0"), T.TN[:, :, 0, :]), (lm("LQ1"), T.TN[:, :, 1, :])], ["MLQ0", "MLQ1", "TN"], ["P5"])
+        cp(T.LN[:], T.P5[:, 0:80], ["P5"], ["LN"])
+        if t < 2:
+            cp(T["AO%d" % e][:, own:own + 160], T.TN[:], ["TN"], ["AO%do" % e], "s")
+            send("o", e)
+        halves = (("wl", 0), ("wr", 1))
+        for k, hf in halves if t < 2 else (halves[1], halves[0]):
+            o, i = T.w[:, 640 * hf:640 * hf + 640], W.indirect(T.LN[:, 40 * hf:40 * hf + 40])
+            cp(o, i, kW + ["LN"], [k], "v" if t < 2 and hf else "s")
+        if t > 0:
+            cp(T.QF[:], T.P5[:, 0:80], ["P5"], ["QF"])
+        ts(T.nd[:], T.TN[:], 79.5, A.is_lt, None, None, ["TN"], ["nd"])
+        mm(T.P6[:, 0:160], [(lm("HA"), T.nd[:])], ["MHA", "nd"], ["P6"])
+        if t == 2:
+            invert(b)
+        tt(T.t1[:, 320:640], T.w[:, 640::2], T.w[:, 641::2], A.max, ["wr"], ["t1r"])
+        tt(T.xx[:], T.P6[:, 0:160], T["xs%d" % b][:], A.add, ["P6", "xs%d" % b], ["xx"])
+        tt(T.t1[:, 0:320], T.w[:, 0:640:2], T.w[:, 1:640:2], A.max, ["wl"], ["t1l"])
+        tt(T.t2[:], T.t1[:, 0::2], T.t1[:, 1::2], A.max, ["t1l", "t1r"], ["t2"])
+        for h in range(2):
+            tt(T.m4[:, :, h, :], T.t2[:, :, :, h, 0], T.t2[:, :, :, h, 1], A.max, ["t2"], ["m4%d" % h])
+        tt(T.mm[:], T.m4[:], T.xx[:], A.max, ["m40", "m41", "xx"], ["mm"])
+        ts(T.nn[:], T.mm[:], -1.0, A.mult, col["tb"], A.add, ["mm", ckey["tb"]], ["nn"])
+        mm(T.P6[:, 0:160], [(lm("P1"), T.nn[:])], ["MP1", "nn"], ["P6"])
+        mm(T.P7[:, 0:160], [(lm("P2"), T.nn[:])], ["MP2", "nn"], ["P7"])
+        cp(T.pp[:], T.P6[:, 0:160], ["P6"], ["pp"], "s")
+        tt(T.qq[:], T.P7[:, 0:160], T.pp[:], A.min, ["P7", "pp"], ["qq"])
+        dst, kd = (T["AW%d" % e][:, own:own + 160], "AW%do" % e) if t < 2 else (T.RF[:], "RF")
+        ts(dst, T.qq[:], MG, A.add, MG, A.subtract, ["qq"], [kd])
+        if t < 2:
+            send("w", e)
+        return dst, kd
+
+    replicate(0)
+    replicate(1)
+    own_walls(1, T.AW1[:, own:own + 160], "AW1o")
+    empties(0, T.eQ[:, 0:80], "eQ")
+    empties(1, T.eQ[:, 80:160], "eQ")
+    dst, kd = rnd(0)
+    mm(T.P4[:, 160:240], [(lm("LQ0s"), T.TN[:, :, 0, :]), (lm("LQ1s"), T.TN[:, :, 1, :])], ["MLQ0s", "MLQ1s", "TN"], ["P4"])
+    for c in range(5):
+        cp(T.LMn[:, c::5], T.P5[:, c * 16:c * 16 + 16], ["P5"], ["LMn"])
+        cp(T.LMs[:, c::5], T.P4[:, 160 + c * 16:176 + c * 16], ["P4"], ["LMs"])
+    ts(T.eQ[:, 0:80], T.LMn[:], 10240.0, A.is_ge, None, None, ["LMn"], ["eQ"])
+    own_walls(0, dst, kd)
+    empties(0, T.eQ[:, 0:80], "eQ")
+    replicate(2)
+    dst, kd = rnd(1)
+    turn_walls(1, dst, kd)
+    invert(1)
+    replicate(3)
+    put_walls(1, "yy")
+    put_slots(1)
+    dst, kd = rnd(2)
+    put_slots(0)
+    turn_walls(0, dst, kd)
+    put_walls(0, "ys")
+    for s in tot:
+        if waited["g"].get(s, 0) < tot[s]:
+            g.wait_ge(T.sem[s], tot[s])

@@ -11,25 +11,25 @@ SCRATCH = {
     "d0": ("sbuf", [128, 160, 2, 2], FB), "d1": ("sbuf", [128, 160, 2, 2], FB),
     "V0": ("sbuf", [128, 160, 2, 2, 2], FB), "V1": ("sbuf", [128, 160, 2, 2, 2], FB),
     "F": ("sbuf", [128, 2304], FB), "EX": ("sbuf", [128, 80, 16], FB),
-    "t1": ("sbuf", [128, 640], FI), "t2": ("sbuf", [128, 5, 16, 2, 2], FI), "m4": ("sbuf", [128, 5, 2, 16], FI),
+    "t1": ("sbuf", [128, 640], FI), "t2": ("sbuf", [128, 5, 8, 2, 2, 2], FI), "m4": ("sbuf", [128, 5, 2, 16], FI),
     "X": ("sbuf", [128, 2, 2, 80], II), "Y": ("sbuf", [128, 2, 2, 80], FI), "TN": ("sbuf", [128, 5, 2, 16], FB),
     "HB": ("sbuf", [128, 2, 5, 16], FB), "LB": ("sbuf", [128, 2, 5, 16], FB), "T4": ("sbuf", [128, 2, 5, 2, 16], FB),
-    "CI": ("sbuf", [128, 16], II), "CF": ("sbuf", [128, 16], FI), "CC": ("sbuf", [128, 48], FI),
+    "CI": ("sbuf", [128, 16], II), "CF": ("sbuf", [128, 16], FI), "CC": ("sbuf", [128, 64], FI),
     "ci": ("sbuf", [128, 143], FI), "kr": ("sbuf", [128, 128], FI), "pr": ("sbuf", [128, 128], FI),
     "DL": ("sbuf", [128, 16], FI), "F9": ("sbuf", [128, 9], FI),
-    "MZ": ("sbuf", [128, 720], FB), "M8": ("sbuf", [128, 1664], FB), "M4": ("sbuf", [128, 896], FI),
+    "MZ": ("sbuf", [128, 720], FB), "M8": ("sbuf", [128, 2688], FB), "M4": ("sbuf", [128, 1408], FI),
 }
-for _n, _w, _t in (("u w x0 x1 AW0 AW1 AW2 AW3", 1280, FI), ("gO cm1 cm2 AO0 AO1 AO2 AO3", 1280, FB), ("bI f1 f2", 256, FI),
-                   ("RAW yi si ti hI lI", 160, II), ("FT dT mT nd", 160, FB), ("LQn LQs", 160, UU),
-                   ("YO C nf tf eQ XO0 XO1 xs0 xs1 xx mm nn pp qq RF", 160, FI), ("LMn LMs L1 L2 LN slU", 80, UU), ("slT", 80, II),
-                   ("eV0 eV1 KC RS H2 kb kb2 g0 g1 gs gm gb sc da RM QF", 80, FI), ("fb cx", 10, FI), ("Mi cd cv", 10, II),
+for _n, _w, _t in (("u x0 x1 AW0 AW1 AW2 AW3", 1280, FI), ("gO cm1 cm2 AO0 AO1 AO2 AO3", 1280, FB), ("bI f1 f2", 256, FI),
+                   ("w", 640, FI), ("RAW yi si0 si1 si2 ti hI lI", 160, II), ("FT dT mT nd", 160, FB), ("LQn LQs", 160, UU),
+                   ("YO C nf tf tf0 tf1 tf2 eQ XO0 XO1 xs0 xs1 xx mm nn pp qq RF", 160, FI), ("LMn LMs L1 L2 LN slU", 80, UU),
+                   ("slT", 80, II), ("KC RS H2 kb kb2 g0 g1 gs gm gb sc da RM QF", 80, FI), ("fb cx", 10, FI), ("Mi cd cv", 10, II),
                    ("iu cu", 10, UU)):
     for _k in _n.split():
         SCRATCH[_k] = ("sbuf", [128, _w], _t)
 for _k in range(8):
     SCRATCH["P%d" % _k] = ("psum", [128, 512], FI)
 SEMAPHORES = ["qv", "qt", "qs", "qg", "ls"] + ["%s%s%d" % (a, b, e) for a in ("rw", "ro") for b in ("n", "f") for e in range(4)] \
-    + ["dm%d" % k for k in range(24)]
+    + ["dm%d" % k for k in range(32)]
 
 
 def rank_program(g, core, T, topo):
@@ -137,8 +137,12 @@ def rank_program(g, core, T, topo):
             tot[sem] = n
             lastw[name + s] = [(sem, n, "x")]
 
+    def wr(sd, G):
+        o = 64 * sd + 32 * (G // 2)
+        return slice(o + G % 2, o + 32, 2)
+
     for q, sd, t, k in (("y", 0, T.lw, "XA"), ("s", 1, T.rw, "XB")):
-        dma(q, [(T.X[64 * sd + G:64 * sd + 64:4, :, h, :], t[16 * (2 * G + h):16 * (2 * G + h) + 16, :])
+        dma(q, [(T.X[wr(sd, G), :, h, :], t[16 * (2 * G + h):16 * (2 * G + h) + 16, :])
                 for G in range(4) for h in range(2)], [], [k])
     dma("y", [(T.RAW[:], T.opts[:])], [], ["RAW"])
 
@@ -151,12 +155,13 @@ def rank_program(g, core, T, topo):
     iota("CI", [[0, 1]], 0, 1)
     iota("ci", [[1, 143]])
     iota("kr", [[16, 2], [0, 4], [1, 16]])
-    names = ["p", "i", "i8", "pg", "sd", "Gp", "xi", "xG", "rs", "g1", "gG", "b0", "b1", "b2"]
-    spec = [None, (0, 15), (0, 7), (4, 7), (6, 1), (4, 3), (2, 15), (0, 3), (3, 1), (4, 1), (5, 3), (0, 1), (1, 1), (2, 1)]
+    names = ["p", "i", "i8", "pg", "sd", "Gp", "xi", "xG", "rs", "g1", "gG", "b0", "b1", "b2", "xh", "Gh"]
+    spec = [None, (0, 15), (0, 7), (4, 7), (6, 1), (4, 3), (1, 15), (0, 1), (3, 1), (4, 1), (5, 3), (0, 1), (1, 1), (2, 1),
+            (5, 1), (5, 1)]
     for k, s in enumerate(spec):
         if s:
             ts(T.CI[:, k:k + 1], T.CI[:, 0:1], s[0], A.logical_shift_right, s[1], A.bitwise_and, ["CI"], ["CI%d" % k])
-    cp(T.CF[:, 0:14], T.CI[:, 0:14], ["CI"] + ["CI%d" % k for k in range(1, 14)], ["CF"])
+    cp(T.CF[:], T.CI[:], ["CI"] + ["CI%d" % k for k in range(1, 16)], ["CF"])
     col = {n: T.CF[:, k:k + 1] for k, n in enumerate(names)}
     ckey = {n: "CF" for n in names}
     nc = [0]
@@ -169,7 +174,10 @@ def rank_program(g, core, T, topo):
         rk = [ckey[src]] + [ckey[s] for s in (s1, s2) if isinstance(s, str)]
         ts(T.CC[:, k:k + 1], col[src], val(s1), o1, val(s2), o2, rk, ["CC%d" % k])
         col[name], ckey[name] = T.CC[:, k:k + 1], "CC%d" % k
-    mk("sgn", "sd", 2.0, A.mult, -1.0, A.add)
+
+    def ma(name, src, m, a):
+        mk(name, src, m, A.mult, a, A.add)
+    ma("sgn", "sd", 2.0, -1.0)
     for b in range(2):
         aw = T["AW%d" % b]
         for c in range(5):
@@ -187,61 +195,32 @@ def rank_program(g, core, T, topo):
     cp(T.yi[:], T.tf[:], ["tf"], ["yi"])
     ts(T.C[:], T.nf[:], 10240.0, A.is_ge, 5120.0, A.mult, ["nf"], ["C"])
 
-    def addterm(acc, x, f, sh, xi, si, tf, kacc, kx):
-        if sh:
-            ts(si, xi, sh, A.logical_shift_right, None, None, [kx], ["si"])
-            ts(tf, si, float(f), A.mult, None, None, ["si"], ["tf"])
-        else:
-            ts(tf, x, float(f), A.mult, None, None, [kx], ["tf"])
-        tt(acc, acc, tf, A.add, [kacc, "tf"], [kacc])
-    addterm(T.C[:], T.nf[:], 32, 0, None, None, T.tf[:], "C", "nf")
-    addterm(T.C[:], T.yi[:], -159, 0, None, None, T.tf[:], "C", "yi")
-    for sh, f in ((4, 5104), (5, -10224), (6, 608), (8, -2400), (10, 1920)):
-        addterm(T.C[:], None, f, sh, T.yi[:], T.si[:], T.tf[:], "C", "yi")
+    def terms(acc, lst, n):
+        st, kacc = [], "C"
+        for j, (f, x, kx, sh) in enumerate(lst):
+            s, t, ks, kt = T["si%d" % (j % 3)][:, 0:n], T["tf%d" % (j % 3)][:, 0:n], "si%d" % (j % 3), "tf%d" % (j % 3)
+            one = [None, (ts, (t, x, float(f), A.mult, None, None, [kx], [kt])), (tt, (acc, acc, t, A.add, [kacc, kt], [kacc]))]
+            if sh:
+                one[0] = (ts, (s, x, sh, A.logical_shift_right, None, None, [kx], [ks]))
+                one[1] = (ts, (t, s, float(f), A.mult, None, None, [ks], [kt]))
+            st += [(2 * j + 3 * k, j, o) for k, o in enumerate(one) if o]
+        return [o for _, _, o in sorted(st, key=lambda z: z[:2])]
+
+    def run(steps):
+        for f, a in steps:
+            f(*a)
+    run(terms(T.C[:], [(32, T.nf[:], "nf", 0), (-159, T.yi[:], "yi", 0)] +
+              [(f, T.yi[:], "yi", sh) for sh, f in ((4, 5104), (5, -10224), (6, 608), (8, -2400), (10, 1920))], 160))
     cp(T.ti[:], T.C[:], ["C"], ["ti"])
     ts(T.hI[:], T.ti[:], 7, A.logical_shift_right, None, None, ["ti"], ["hI"])
     ts(T.lI[:], T.ti[:], 127, A.bitwise_and, None, None, ["ti"], ["lI"])
     for c in range(5):
         cp(T.HB[:, :, c, :], T.hI[:, c::5], ["hI"], ["HB%d" % c])
         cp(T.LB[:, :, c, :], T.lI[:, c::5], ["lI"], ["LB%d" % c])
-    mk("lo", "i", 8.0, A.is_ge)
-    mk("w", "lo", -127.0, A.mult, 128.0, A.add)
-    mk("wn", "lo", -1.0, A.mult, 1.0, A.add)
-    mk("hbw", "wn", -BIG, A.mult)
-    mk("e80", "wn", 80.0, A.mult)
-    mk("sw", "sd", -128.0, A.mult, 64.0, A.add)
-    mk("swr", "rs", -128.0, A.mult, 64.0, A.add)
-    mk("tz", "pg", 16.0, A.mult, 15.0, A.add)
-    mk("tzs", "tz", "sw", A.add)
-    mk("tl0", "pg", 16.0, A.mult, "i8", A.add)
-    mk("tl1", "tl0", 8.0, A.add)
-    mk("tl0s", "tl0", "sw", A.add)
-    mk("tl1s", "tl1", "sw", A.add)
-    mk("a1", "i", 4.0, A.mult, "pg", A.add)
-    mk("tp", "sd", 60.0, A.mult, "a1", A.add)
-    mk("tps", "tp", "sw", A.add)
-    mk("a2", "xG", 16.0, A.mult, "xi", A.add)
-    mk("xst", "sd", 64.0, A.mult, "a2", A.add)
-    mk("xot", "xst", "sw", A.add)
-    mk("a3", "pg", 8.0, A.mult, "i8", A.add)
-    mk("qt", "rs", 64.0, A.mult, "a3", A.add)
-    mk("qst", "qt", "swr", A.add)
-    mk("a4", "gG", 16.0, A.mult, "i8", A.add)
-    mk("th", "rs", 64.0, A.mult, "a4", A.add)
+    ma("a4", "gG", 16.0, "i8")
+    ma("th", "rs", 64.0, "a4")
     mk("tlo", "th", 8.0, A.add)
-    mk("m0", "g1", -1.0, A.mult, 1.0, A.add)
-    mk("kc", "sd", 16.0, A.mult, "i", A.add)
-    for k in range(4):
-        mk("mG%d" % k, "Gp", float(k), A.is_equal)
-    mk("tm", "i", 1024.0, A.mult)
-    mk("a5", "sd", -0.5, A.mult, 0.25, A.add)
-    mk("tb", "tm", "a5", A.add)
-    mk("a6", "b1", 3.0, A.mult, 1.0, A.add)
-    mk("a7", "b2", 15.0, A.mult, 1.0, A.add)
-    mk("a8", "b0", 1.0 / 128, A.mult, 1.0 / 128, A.add)
-    mk("a9", "a8", "a6", A.mult)
-    mk("c1", "a9", "a7", A.mult)
-    mk("s8", "i8", -1.0, A.mult, 8.0, A.add)
+    ma("m0", "g1", -1.0, 1.0)
 
     mats = {}
 
@@ -273,18 +252,97 @@ def rank_program(g, core, T, topo):
             cp(T.T4[:, b, :, h, :], T.P6[:, o:o + 80], ["P6"], ["T4%d%d" % (b, h)])
         cp(T["AO%d" % b][:, own:own + 160], T.T4[:, b, :, :, :], ["T4%d0" % b, "T4%d1" % b], ["AO%do" % b])
         send("o", b)
+    ma("swr", "rs", -128.0, 64.0)
+    ma("a3", "pg", 8.0, "i8")
+    ma("qt", "rs", 64.0, "a3")
+    mk("qst", "qt", "swr", A.add)
+    ma("kc", "sd", 16.0, "i")
+    ma("xq", "xh", 2.0, "xG")
+    ma("kw", "sd", -16.0, 16.0)
+    mk("kcw", "kw", "xi", A.add)
+    for k in range(4):
+        mk("mG%d" % k, "Gp", float(k), A.is_equal)
+        mk("mX%d" % k, "xq", float(k), A.is_equal)
     mat("QN", "M4", 0, 128, 128, c128, "ci", "qt", 1.0)
     mat("QS", "M4", 1, 128, 128, c128, "ci", "qst", 1.0)
     mm(T.P5[:, 0:160], [(lm("QN"), T.C[:])], ["MQN", "C"], ["P5"])
     mm(T.P5[:, 160:320], [(lm("QS"), T.C[:])], ["MQS", "C"], ["P5"])
     cp(T.LQn[:], T.P5[:, 0:160], ["P5"], ["LQn"])
     cp(T.LQs[:], T.P5[:, 160:320], ["P5"], ["LQs"])
-    ts(T.eQ[:], T.P5[:, 0:160], 10240.0, A.is_ge, None, None, ["P5"], ["eQ"])
+    ts(T.eQ[:], T.P5[:, 0:160], 10240.0, A.is_ge, None, None, ["P5"], ["eQ0"])
+    lastw["eQ1"] = lastw["eQ0"]
+    for k in range(4):
+        mat("WG%d" % k, "M4", 7 + k, 128, 128, T.kr[:], "kr", "kcw", "mX%d" % k)
+        mat("RG%d" % k, "M8", 4 + k, 128, 128, T.kr[:], "kr", "kc", "mG%d" % k)
+
+    turn = [0]
+
+    def through(e, H, out, okey, tile, tkeys, m, eng, Gs=(0, 1, 2, 3)):
+        for G in Gs:
+            for k in range(2):
+                pk = "P%d" % (turn[0] % 4)
+                o = (e % 2) * 5120 + H * 2560 + G * 640 + k * 320
+                mm(T[pk][:, 0:320], [(lm("%s%d" % (m, G)), tile[:, H * 640 + k * 320:H * 640 + k * 320 + 320])],
+                   ["M%s%d" % (m, G)] + tkeys, [pk])
+                cp(out[:, o:o + 320], T[pk][:, 0:320], [pk], ["%s%d" % (okey, o)], eng[turn[0] % 2])
+                turn[0] += 1
+
+    def slots_in(e, eng):
+        for H in (nearH, 1 - nearH):
+            through(e, H, T.OT, "OT", T["AO%d" % e], ["AO%do" % e, "AO%dn" % e] if H == nearH else ["AO%df" % e], "RG", eng)
+
+    def walls_pe(e, eng):
+        through(e, nearH, T.W, "W", T["AW%d" % e], ["AW%do" % e, "AW%dn" % e], "WG", eng, (0, 1))
+
+    def walls_dma(e, H, halves):
+        aw = T["AW%d" % e]
+        for u in halves:
+            c0 = (e % 2) * 5120 + H * 2560 + u * 1280
+            dma("y", [(T.W[16 * q:16 * q + 16, c0:c0 + 1280],
+                       aw[(64 if q < 4 else 0) + 32 * u:(96 if q < 4 else 32) + 32 * u, H * 640:H * 640 + 640])
+                      for q in range(8)], ["AW%do" % e, "AW%dn" % e] if H == nearH else ["AW%df" % e],
+                ["W%d" % (c0 + 320 * k) for k in range(4)])
+    for e in range(2):
+        walls_dma(e, nearH, (1,))
+        walls_dma(e, 1 - nearH, (0, 1))
+    walls_pe(0, "ss")
+    walls_pe(1, "ss")
+    slots_in(0, "ss")
+    mk("lo", "i", 8.0, A.is_ge)
+    ma("w", "lo", -127.0, 128.0)
+    ma("wn", "lo", -1.0, 1.0)
+    mk("hbw", "wn", -BIG, A.mult)
+    mk("e80", "wn", 80.0, A.mult)
+    ma("sw", "sd", -128.0, 64.0)
+    ma("tz", "pg", 16.0, 15.0)
+    mk("tzs", "tz", "sw", A.add)
+    ma("tl0", "pg", 16.0, "i8")
+    mk("tl1", "tl0", 8.0, A.add)
+    mk("tl0s", "tl0", "sw", A.add)
+    mk("tl1s", "tl1", "sw", A.add)
+    ma("a0", "i", 2.0, "g1")
+    ma("a1", "Gh", 32.0, "a0")
+    ma("tp", "sd", 64.0, "a1")
+    mk("tps", "tp", "sw", A.add)
+    ma("a2", "xq", 16.0, "xi")
+    ma("xst", "sd", 64.0, "a2")
+    mk("xot", "xst", "sw", A.add)
+    mk("tm", "i", 1024.0, A.mult)
+    mk("w1", "b2", "w", A.mult)
+    mk("w0", "w", "w1", A.subtract)
+    ma("t2", "b2", -4.0, "i8")
+    ma("t3", "pg", 16.0, "t2")
+    ma("a5", "sd", -0.5, 0.25)
+    mk("tb", "tm", "a5", A.add)
+    ma("a6", "b1", 3.0, 1.0)
+    ma("a7", "b2", 15.0, 1.0)
+    ma("a8", "b0", 1.0 / 128, 1.0 / 128)
+    mk("a9", "a8", "a6", A.mult)
+    mk("c1", "a9", "a7", A.mult)
+    ma("s8", "i8", -1.0, 8.0)
     op("v", lambda e: e.memset(T.W[:, E:E + 8], -BIG), [], ["We"])
     op("v", lambda e: e.memset(T.OT[:, E:E + 16], 0.0), [], ["OTz"])
     cp(T.OT[:, E:E + 1], col["e80"], [ckey["e80"], "OTz"], ["OTe"])
-    for k in range(4):
-        mat("RG%d" % k, "M8", 4 + k, 128, 128, T.kr[:], "kr", "kc", "mG%d" % k)
     ts(T.slU[:], T.slT[:], col["i"], A.add, None, None, ["slT", "CF"], ["slU"])
     mat("XO", "M4", 2, 128, 128, c128, "ci", "xot", 1.0)
     mat("XS", "M4", 3, 128, 128, c128, "ci", "xst", -1.0)
@@ -295,7 +353,6 @@ def rank_program(g, core, T, topo):
         cp(T["XO%d" % b][:], T.P7[:, 0:160], ["P7"], ["XO%d" % b])
         ts(T["xs%d" % b][:], T.P7[:, 160:320], col["tm"], A.add, None, None, ["P7", ckey["tm"]], ["xs%d" % b])
         cp(T["x%d" % b][:], T["XO%d" % b][:].indirect(T.slU[:]), ["XO%d" % b, "slU"], ["x%d" % b], "s")
-    own_walls(0, T.AW0[:, own:own + 160], "AW0o")
     zk = (("ZKs", "tzs", "w"), ("ZK", "tz", "w"), ("Z1", "tz", 1.0), ("ZV", "tz", -262144.0), ("ZVs", "tzs", -262144.0))
     for k, (n, t, m) in enumerate(zk):
         mat(n, "MZ", k, 143, 144, T.ci[:], "ci", t, m)
@@ -305,12 +362,11 @@ def rank_program(g, core, T, topo):
     ts(T.RS[:], T.RS[:], 0.5, A.is_gt, None, None, ["RS"], ["RS"])
     ts(T.H2[:], T.RS[:], 2.0, A.mult, None, None, ["RS"], ["H2"])
 
-    def empties(b, eq, keq):
+    def empties(eq, keq):
         for k in range(16):
             op("s", lambda e: e.activation(T.EX[:, :, k], eq, AF.Identity, scale=T.DL[:, k:k + 1]), [keq, "DL"], ["EX%d" % k])
-        mm(T.P4[:, 0:80], [(lz("Z1", a), T.EX[:, 5 * a:5 * a + 5, :]) for a in range(16)],
-           ["MZ1"] + ["EX%d" % k for k in range(16)], ["P4"])
-        cp(T["eV%d" % b][:], T.P4[:, 0:80], ["P4"], ["eV%d" % b])
+        mm(T.P5[:, 0:80], [(lz("Z1", a), T.EX[:, 5 * a:5 * a + 5, :]) for a in range(16)],
+           ["MZ1"] + ["EX%d" % k for k in range(16)], ["P5"])
     for dst, sc in (("f1", 1.0), ("f2", 0.5)):
         ts(T[dst][:], T.bI[:], col["c1"], A.mult, sc, A.mult, ["bI", ckey["c1"]], [dst])
         ts(T[dst][:], T[dst][:], -0.5 + 2.0 ** -9, A.add, None, None, [dst], [dst])
@@ -321,53 +377,32 @@ def rank_program(g, core, T, topo):
     for k in range(9):
         ts(T.F[:, k::9], T.f1[:], T.F9[:, k:k + 1], A.max, None, None, ["f1", "F9"], ["F%d" % k])
     kF = ["F%d" % k for k in range(9)]
-    for k, (n, t, m) in enumerate((("LQ0", "tl0", "w"), ("LQ1", "tl1", "w"), ("LQ0s", "tl0s", "w"), ("LQ1s", "tl1s", "w"))):
-        mat(n, "M8", 8 + k, 128, 128, c128, "ci", t, m)
+    for k, (n, t) in enumerate((("LQ0", "tl0"), ("LQ1", "tl1"), ("LQ0s", "tl0s"), ("LQ1s", "tl1s"))):
+        mat(n, "M8", 8 + k, 128, 128, c128, "ci", t, "w")
+    for h in range(2):
+        for n in range(2):
+            mk("tn%d%d" % (h, n), "t3", 8.0 * h + 4.0 * n, A.add)
+            for k in range(2):
+                mat("LN%d%d%d" % (h, n, k), "M8", 13 + 4 * h + 2 * n + k, 128, 128, c128, "ci", "tn%d%d" % (h, n), "w%d" % k)
     mat("HA", "M8", 12, 128, 128, T.pr[:], "pr", "pg", "hbw")
     mat("P1", "M4", 4, 128, 128, c128, "ci", "tp", 1.0)
     mat("P2", "M4", 5, 128, 128, c128, "ci", "tp", 0.5)
     mat("P3", "M4", 6, 128, 128, c128, "ci", "tps", -0.5)
     tt(lm("P2"), lm("P2"), lm("P3"), A.add, ["MP2", "MP3"], ["MP2"])
 
-    turn = [0]
-
-    def replicate(e):
-        b = e % 2
-        aw, ao = T["AW%d" % e], T["AO%d" % e]
-        for H in (nearH, 1 - nearH):
-            kw = ["AW%do" % e, "AW%dn" % e] if H == nearH else ["AW%df" % e]
-            ko = ["AO%do" % e, "AO%dn" % e] if H == nearH else ["AO%df" % e]
-            c0 = b * 5120 + H * 2560
-            dma("y", [(T.W[16 * q:16 * q + 16, c0:c0 + 2560], aw[(64 if q < 4 else 0):(128 if q < 4 else 64), H * 640:H * 640 + 640])
-                      for q in range(8)], kw, ["W%d%d" % (b, H)])
-            for G in range(4):
-                for k in range(2):
-                    pk = "P%d" % (turn[0] % 4)
-                    o = c0 + G * 640 + k * 320
-                    mm(T[pk][:, 0:320], [(lm("RG%d" % G), ao[:, H * 640 + k * 320:H * 640 + k * 320 + 320])],
-                       ["MRG%d" % G] + ko, [pk])
-                    cp(T.OT[:, o:o + 320], T[pk][:, 0:320], [pk], ["OT%d" % o], "v" if turn[0] % 2 else "s")
-                    turn[0] += 1
-    kW = ["We"] + ["W%d%d" % (b, H) for b in range(2) for H in range(2)]
+    kW = ["We"] + ["W%d" % (320 * k) for k in range(32)]
     kOT = ["OTe"] + ["OT%d" % (320 * k) for k in range(32)]
     W, OT = T.W[:, 0:E + 8], T.OT[:, 0:E + 16]
 
     def invert(b):
-        f, i, s, t = T.nf[:, 0:80], T.ti[:, 0:80], T.si[:, 0:80], T.tf[:, 0:80]
+        f, i, v = T.nf[:, 0:80], T.ti[:, 0:80], T.hI[:, 0:80]
         acc, y = T.C[:, 0:80], T.yi[:, 0:80]
-        cp(i, T.QF[:], ["QF"], ["ti"])
-        ts(acc, T.QF[:], 10240.0, A.is_ge, 10080.0, A.mult, ["QF"], ["C"])
-        addterm(acc, T.QF[:], 5, 0, None, None, t, "C", "QF")
-        addterm(acc, None, 80, 4, i, s, t, "C", "ti")
-        addterm(acc, None, -319, 5, i, s, t, "C", "ti")
-        ts(s, i, 5, A.logical_shift_right, None, None, ["ti"], ["si"])
-        ts(f, s, 0.2, A.mult, -0.4, A.add, ["si"], ["nf"])
-        cp(y, f, ["nf"], ["yi"])
-        addterm(acc, y, 1275, 0, None, None, t, "C", "yi")
-        for sh, k in ((2, -4800), (4, 3840), (5, -10160)):
-            addterm(acc, None, k, sh, y, s, t, "C", "yi")
-        for c in range(5):
-            cp(T.YO[:, b * 80 + c:b * 80 + 80:5], T.C[:, c * 16:c * 16 + 16], ["C"], ["YO%d" % b])
+        a = [(cp, (i, T.QF[:], ["QF"], ["ti"])), (ts, (acc, T.QF[:], 10240.0, A.is_ge, 10080.0, A.mult, ["QF"], ["C"])),
+             (ts, (v, i, 5, A.logical_shift_right, None, None, ["ti"], ["hI"])),
+             (ts, (f, v, 0.2, A.mult, -0.4, A.add, ["hI"], ["nf"])), (cp, (y, f, ["nf"], ["yi"]))]
+        a += terms(acc, [(5, T.QF[:], "QF", 0), (80, i, "ti", 4), (-319, i, "ti", 5), (1275, y, "yi", 0)] +
+                   [(k, y, "yi", sh) for sh, k in ((2, -4800), (4, 3840), (5, -10160))], 80)
+        return a + [(cp, (T.YO[:, b * 80 + c:b * 80 + 80:5], T.C[:, c * 16:c * 16 + 16], ["C"], ["YO%d" % b])) for c in range(5)]
 
     def put_slots(b):
         dma("y", [(T.yo[16 * gg + 8 * sd:16 * gg + 8 * sd + 8, b * 80:b * 80 + 80],
@@ -380,7 +415,7 @@ def rank_program(g, core, T, topo):
 
     def put_walls(b, qs):
         for sd, o in ((0, T.yl), (1, T.yr)):
-            dma(qs[sd], [(o[16 * (2 * G + h):16 * (2 * G + h) + 16, b * 80:b * 80 + 80], T.Y[64 * sd + G:64 * sd + 64:4, b, h, :])
+            dma(qs[sd], [(o[16 * (2 * G + h):16 * (2 * G + h) + 16, b * 80:b * 80 + 80], T.Y[wr(sd, G), b, h, :])
                          for G in range(4) for h in range(2)], ["Y%d" % b], [])
 
     def rnd(t):
@@ -389,6 +424,7 @@ def rank_program(g, core, T, topo):
         lqn = (T.LQn[:, b * 80:b * 80 + 80], T.LQs[:, b * 80:b * 80 + 80]) if t < 2 else (T.LMn[:], T.LMs[:])
         kl = ("LQn", "LQs") if t < 2 else ("LMn", "LMs")
         x, kx = T["x%d" % b][:], "x%d" % b
+        empties(T.eQ[:, 80 * b:80 * b + 80], "eQ%d" % b)
         op("s", lambda q: q.activation(T.u[:], W.indirect(lqn[0]), AF.Identity), kW + [kl[0]], ["u"])
         op("v", lambda q: q.tensor_tensor(T.gO[:], OT.indirect(lqn[1]), T.MB[:, 16 * t:16 * t + 1280], A.mult), kOT + [kl[1], "MB"], ["gO"])
         mm(T.P0[:, 0:80], [(lz("ZKs", a), T.gO[:, 80 * a:80 * a + 80]) for a in range(16)], ["MZKs", "gO"], ["P0"])
@@ -438,36 +474,35 @@ def rank_program(g, core, T, topo):
             mm(T["P%d" % (2 + q)][:, 0:80], [(lz("Z1", a), T["V%d" % q][:, 10 * a:10 * a + 10, :, :, :]) for a in range(16)],
                ["MZ1", "V%d" % q], ["P%d" % (2 + q)])
 
-        def gone(q):
-            m, gt, gk = ms[q], T["g%d" % q], "g%d" % q
-            hb = m.bit_length() - 1
-            ts(gt[:], T["P%d" % (2 + q)][:, 0:80], 0.5, A.is_lt, None, None, ["P%d" % (2 + q)], [gk])
-            need("v", [gk], [])
-            for k in range(1 << hb):
-                op("v", lambda qq: qq.tensor_tensor(gt[:, k::2 << hb], gt[:, k::2 << hb], gt[:, (k ^ m)::2 << hb], A.is_gt))
-            done(("qv", tot["qv"], "v"), [], [gk])
-        diffs(0)
-        parts(0)
+        def gone():
+            for q in range(2):
+                ts(T["g%d" % q][:], T["P%d" % (2 + q)][:, 0:80], 0.5, A.is_lt, None, None, ["P%d" % (2 + q)], ["g%d" % q])
+            for q in range(2):
+                gt, gk, m = T["g%d" % q], "g%d" % q, ms[q]
+                st = 2 << (m.bit_length() - 1)
+                need("v", [gk], [])
+                for k in range(st // 2):
+                    op("v", lambda qq: qq.tensor_tensor(gt[:, k::st], gt[:, k::st], gt[:, (k ^ m)::st], A.is_gt))
+                done(("qv", tot["qv"], "v"), [], [gk])
         cp(T.L1[:], T.P0[:, 0:80], ["P0"], ["L1"])
-        op("v", lambda q: q.tensor_tensor(T.cm1[:], W.indirect(T.L1[:]), x, A.is_gt), kW + ["L1", kx], ["cm1"])
-        sums(0)
-        mm(T.P4[:, 0:80], [(lz("ZV", a), T.cm1[:, a::16]) for a in range(16)], ["MZV", "cm1"], ["P4"], True, False)
         cp(T.L2[:], T.P1[:, 0:80], ["P1"], ["L2"])
-        diffs(1)
-        parts(1)
+        op("v", lambda q: q.tensor_tensor(T.cm1[:], W.indirect(T.L1[:]), x, A.is_gt), kW + ["L1", kx], ["cm1"])
+        mm(T.P4[:, 0:80], [(lz("ZV", a), T.cm1[:, a::16]) for a in range(16)], ["MZV", "cm1"], ["P4"], True, False)
+        for q in range(2):
+            diffs(q)
+            parts(q)
+            sums(q)
         op("v", lambda q: q.tensor_tensor(T.cm2[:], W.indirect(T.L2[:]), x, A.is_lt), kW + ["L2", kx], ["cm2"])
-        sums(1)
         mm(T.P4[:, 0:80], [(lz("ZVs", a), T.cm2[:, a::16]) for a in range(16)], ["MZVs", "cm2"], ["P4"], False, True)
         tt(T.kb[:], T.KC[:], T.P0[:, 0:80], A.subtract, ["KC", "P0"], ["kb"])
-        gone(0)
-        gone(1)
+        gone()
         tt(T.gs[:], T.g0[:], T.g1[:], A.max, ["g0", "g1"], ["gs"])
         ts(T.gm[:], T.gs[:], -262144.0, A.mult, None, None, ["gs"], ["gm"])
-        tt(T.gb[:], T.gs[:], T["eV%d" % b][:], A.max, ["gs", "eV%d" % b], ["gb"])
+        tt(T.gb[:], T.P5[:, 0:80], T.gs[:], A.max, ["gs", "P5"], ["gb"])
         tt(T.kb2[:], T.kb[:], T.gm[:], A.add, ["kb", "gm"], ["kb2"])
         op("v", lambda q: q.tensor_tensor_scan(T.sc[:], T.H2[:], T.gb[:], 0.0, A.mult, A.add), ["H2", "gb"], ["sc"])
-        ts(T.fb[:], T.sc[:, 7::8], 9.0, A.mult, None, None, ["sc"], ["fb"])
         tt(T.da[:], T.P4[:, 0:80], T.kb2[:], A.add, ["P4", "kb2"], ["da"])
+        ts(T.fb[:], T.sc[:, 7::8], 9.0, A.mult, None, None, ["sc"], ["fb"])
         op("v", lambda q: q.tensor_tensor_scan(T.RM[:], T.RS[:], T.da[:], 0.0, A.mult, A.max), ["RS", "da"], ["RM"])
         cp(T.Mi[:], T.RM[:, 7::8], ["RM"], ["Mi"])
         ts(T.cd[:], T.Mi[:], 14, A.logical_shift_right, None, None, ["Mi"], ["cd"])
@@ -480,63 +515,71 @@ def rank_program(g, core, T, topo):
         op("v", lambda q: q.tensor_tensor(T.dT[:], OT.indirect(T.cu[:]), old, A.subtract), kOT + ["cu", ko], ["dT"])
         tt(T.mT[:], T.dT[:], T.FT[:], A.mult, ["dT", "FT"], ["mT"])
         tt(T.TN[:], T.mT[:], old, A.add, ["mT", ko], ["TN"])
-        mm(T.P5[:, 0:80], [(lm("LQ0"), T.TN[:, :, 0, :]), (lm("LQ1"), T.TN[:, :, 1, :])], ["MLQ0", "MLQ1", "TN"], ["P5"])
+        for k in range(2):
+            mm(T.P5[:, 40 * k:40 * k + 40], [(lm("LN%d%d%d" % (h, n, k)), T.TN[:, :, h, n::2]) for h in range(2) for n in range(2)],
+               ["MLN%d%d%d" % (h, n, k) for h in range(2) for n in range(2)] + ["TN"], ["P5"])
         cp(T.LN[:], T.P5[:, 0:80], ["P5"], ["LN"])
         if t < 2:
             cp(T["AO%d" % e][:, own:own + 160], T.TN[:], ["TN"], ["AO%do" % e], "s")
             send("o", e)
-        halves = (("wl", 0), ("wr", 1))
-        for k, hf in halves if t < 2 else (halves[1], halves[0]):
-            o, i = T.w[:, 640 * hf:640 * hf + 640], W.indirect(T.LN[:, 40 * hf:40 * hf + 40])
-            cp(o, i, kW + ["LN"], [k], "v" if t < 2 and hf else "s")
+        mm(T.P4[:, 160:240], [(lm("LQ0"), T.TN[:, :, 0, :]), (lm("LQ1"), T.TN[:, :, 1, :])], ["MLQ0", "MLQ1", "TN"], ["P4"])
+        for k in range(2):
+            cp(T.w[:, 320 * k:320 * k + 320], W.indirect(T.LN[:, 20 * k:20 * k + 20]), kW + ["LN"], ["w%d" % k], "s")
+        inv = []
         if t > 0:
-            cp(T.QF[:], T.P5[:, 0:80], ["P5"], ["QF"])
+            cp(T.QF[:], T.P4[:, 160:240], ["P4"], ["QF"])
+            inv = invert(b) if t == 2 else []
         ts(T.nd[:], T.TN[:], 79.5, A.is_lt, None, None, ["TN"], ["nd"])
+        run(inv[0:5])
         mm(T.P6[:, 0:160], [(lm("HA"), T.nd[:])], ["MHA", "nd"], ["P6"])
-        if t == 2:
-            invert(b)
-        tt(T.t1[:, 320:640], T.w[:, 640::2], T.w[:, 641::2], A.max, ["wr"], ["t1r"])
+        for k in range(2):
+            o = 320 * k
+            op("v", lambda q: q.tensor_tensor(T.t1[:, o:o + 320], W.indirect(T.LN[:, 40 + 20 * k:60 + 20 * k]), T.w[:, o:o + 320], A.max),
+               kW + ["LN", "w%d" % k], ["t1%d" % k])
         tt(T.xx[:], T.P6[:, 0:160], T["xs%d" % b][:], A.add, ["P6", "xs%d" % b], ["xx"])
-        tt(T.t1[:, 0:320], T.w[:, 0:640:2], T.w[:, 1:640:2], A.max, ["wl"], ["t1l"])
-        tt(T.t2[:], T.t1[:, 0::2], T.t1[:, 1::2], A.max, ["t1l", "t1r"], ["t2"])
+        tt(T.t2[:], T.t1[:, 0::2], T.t1[:, 1::2], A.max, ["t10", "t11"], ["t2"])
         for h in range(2):
-            tt(T.m4[:, :, h, :], T.t2[:, :, :, h, 0], T.t2[:, :, :, h, 1], A.max, ["t2"], ["m4%d" % h])
-        tt(T.mm[:], T.m4[:], T.xx[:], A.max, ["m40", "m41", "xx"], ["mm"])
+            for n in range(2):
+                tt(T.m4[:, :, h, n::2], T.t2[:, :, :, h, n, 0], T.t2[:, :, :, h, n, 1], A.max, ["t2"], ["m4%d%d" % (h, n)])
+        tt(T.mm[:], T.m4[:], T.xx[:], A.max, ["m400", "m401", "m410", "m411", "xx"], ["mm"])
         ts(T.nn[:], T.mm[:], -1.0, A.mult, col["tb"], A.add, ["mm", ckey["tb"]], ["nn"])
         mm(T.P6[:, 0:160], [(lm("P1"), T.nn[:])], ["MP1", "nn"], ["P6"])
         mm(T.P7[:, 0:160], [(lm("P2"), T.nn[:])], ["MP2", "nn"], ["P7"])
+        run(inv[5:13])
         cp(T.pp[:], T.P6[:, 0:160], ["P6"], ["pp"], "s")
         tt(T.qq[:], T.P7[:, 0:160], T.pp[:], A.min, ["P7", "pp"], ["qq"])
         dst, kd = (T["AW%d" % e][:, own:own + 160], "AW%do" % e) if t < 2 else (T.RF[:], "RF")
         ts(dst, T.qq[:], MG, A.add, MG, A.subtract, ["qq"], [kd])
         if t < 2:
             send("w", e)
-        return dst, kd
+        return dst, kd, inv[13:]
 
-    replicate(0)
-    replicate(1)
+    own_walls(0, T.AW0[:, own:own + 160], "AW0o")
+    slots_in(1, "sv")
+    dst, kd, inv = rnd(0)
     own_walls(1, T.AW1[:, own:own + 160], "AW1o")
-    empties(0, T.eQ[:, 0:80], "eQ")
-    empties(1, T.eQ[:, 80:160], "eQ")
-    dst, kd = rnd(0)
-    mm(T.P4[:, 160:240], [(lm("LQ0s"), T.TN[:, :, 0, :]), (lm("LQ1s"), T.TN[:, :, 1, :])], ["MLQ0s", "MLQ1s", "TN"], ["P4"])
+    mm(T.P4[:, 240:320], [(lm("LQ0s"), T.TN[:, :, 0, :]), (lm("LQ1s"), T.TN[:, :, 1, :])], ["MLQ0s", "MLQ1s", "TN"], ["P4"])
     for c in range(5):
-        cp(T.LMn[:, c::5], T.P5[:, c * 16:c * 16 + 16], ["P5"], ["LMn"])
-        cp(T.LMs[:, c::5], T.P4[:, 160 + c * 16:176 + c * 16], ["P4"], ["LMs"])
-    ts(T.eQ[:, 0:80], T.LMn[:], 10240.0, A.is_ge, None, None, ["LMn"], ["eQ"])
+        cp(T.LMn[:, c::5], T.P4[:, 160 + c * 16:176 + c * 16], ["P4"], ["LMn"])
+        cp(T.LMs[:, c::5], T.P4[:, 240 + c * 16:256 + c * 16], ["P4"], ["LMs"])
+    ts(T.eQ[:, 0:80], T.LMn[:], 10240.0, A.is_ge, None, None, ["LMn"], ["eQ0"])
     own_walls(0, dst, kd)
-    empties(0, T.eQ[:, 0:80], "eQ")
-    replicate(2)
-    dst, kd = rnd(1)
+    for H in (nearH, 1 - nearH):
+        walls_dma(2, H, (0, 1))
+    slots_in(2, "sv")
+    dst, kd, inv = rnd(1)
     turn_walls(1, dst, kd)
-    invert(1)
-    replicate(3)
+    run(invert(1))
+    for H in (nearH, 1 - nearH):
+        walls_dma(3, H, (0, 1))
+    slots_in(3, "sv")
     put_walls(1, "yy")
     put_slots(1)
-    dst, kd = rnd(2)
-    put_slots(0)
+    dst, kd, inv = rnd(2)
     turn_walls(0, dst, kd)
     put_walls(0, "ys")
+    run(inv)
+    put_slots(0)
     for s in tot:
         if waited["g"].get(s, 0) < tot[s]:
             g.wait_ge(T.sem[s], tot[s])

from concourse.bass import DstId, RemoteDMATransfer
from concourse.mybir import AluOpType as A, ActivationFunctionType as AF

N, V, B, E = 8, 160, 80, 10240
BIG = 8388608.0
MG = 12582912.0
FI, FB, II, UU = "float32", "bfloat16", "int32", "uint16"
SCRATCH = {
    "W": ("sbuf", [128, E + 8], FI), "OT": ("sbuf", [128, E + 16], FB),
    "MB": ("sbuf", [128, 1312], FB), "mI": ("sbuf", [128, 1312], II),
    "d0": ("sbuf", [128, 160, 2, 2], FB), "d1": ("sbuf", [128, 160, 2, 2], FB),
    "V0": ("sbuf", [128, 160, 2, 2, 2], FB), "V1": ("sbuf", [128, 160, 2, 2, 2], FB),
    "F": ("sbuf", [128, 2304], FB), "EX": ("sbuf", [128, 80, 16], FB),
    "t1": ("sbuf", [128, 640], FI), "t2": ("sbuf", [128, 5, 8, 2, 2, 2], FI), "m4": ("sbuf", [128, 5, 2, 16], FI),
    "X": ("sbuf", [128, 2, 2, 80], II), "Y": ("sbuf", [128, 2, 2, 80], FI), "TN": ("sbuf", [128, 5, 2, 16], FB),
    "HB": ("sbuf", [128, 2, 5, 16], FB), "LB": ("sbuf", [128, 2, 5, 16], FB), "T4": ("sbuf", [128, 2, 5, 2, 16], FB),
    "CI": ("sbuf", [128, 16], II), "CF": ("sbuf", [128, 16], FI), "CC": ("sbuf", [128, 64], FI),
    "ci": ("sbuf", [128, 143], FI), "kr": ("sbuf", [128, 128], FI), "pr": ("sbuf", [128, 128], FI),
    "DL": ("sbuf", [128, 16], FI), "F9": ("sbuf", [128, 9], FI),
    "MZ": ("sbuf", [128, 720], FB), "M8": ("sbuf", [128, 2688], FB), "M4": ("sbuf", [128, 1408], FI),
}
for _n, _w, _t in (("u x0 x1 AW0 AW1 AW2 AW3", 1280, FI), ("gO cm1 cm2 AO0 AO1 AO2 AO3", 1280, FB), ("bI f1 f2", 256, FI),
                   ("w", 640, FI), ("RAW yi si0 si1 si2 ti hI lI", 160, II), ("FT dT mT nd", 160, FB), ("LQn LQs", 160, UU),
                   ("YO C nf tf tf0 tf1 tf2 eQ XO0 XO1 xs0 xs1 xx mm nn pp qq RF", 160, FI), ("LMn LMs L1 L2 LN slU", 80, UU),
                   ("slT", 80, II), ("KC RS H2 kb kb2 g0 g1 gs gm gb sc da RM QF", 80, FI), ("fb cx", 10, FI), ("Mi cd cv", 10, II),
                   ("iu cu", 10, UU)):
    for _k in _n.split():
        SCRATCH[_k] = ("sbuf", [128, _w], _t)
for _k in range(8):
    SCRATCH["P%d" % _k] = ("psum", [128, 512], FI)
SEMAPHORES = ["qv", "qt", "qs", "qg", "ls"] + ["%s%s%d" % (a, b, e) for a in ("rw", "ro") for b in ("n", "f") for e in range(4)] \
    + ["dm%d" % k for k in range(32)]


def rank_program(g, core, T, topo):
    rank = T.rank_of(core)
    if rank is None:
        return
    QU = {"v": g.vector, "t": g.tensor, "s": g.scalar, "g": g, "y": g.sync}
    tot = {}
    waited = {q: {} for q in QU}
    lastw, lastr = {}, {}
    ndma = [0]

    def wait(q, tok):
        sem, val, tq = tok
        if waited[q].get(sem, 0) < val:
            QU[q].wait_ge(T.sem[sem], val)
            waited[q][sem] = val

    def need(q, r, w):
        for k in r:
            for t in lastw.get(k, []):
                wait(q, t)
            if k[0] == "P":
                for t in lastr.get(k, []):
                    if t[2] != q:
                        wait(q, t)
        for k in w:
            for t in lastw.get(k, []) + lastr.get(k, []):
                if not (q == "t" and t[2] == "t"):
                    wait(q, t)

    def done(tok, r, w):
        for k in r:
            lastr.setdefault(k, []).append(tok)
        for k in w:
            lastw[k], lastr[k] = [tok], []

    def op(q, fn, r=(), w=()):
        need(q, r, w)
        s = "q" + q
        tot[s] = tot.get(s, 0) + 1
        fn(QU[q]).then_inc(T.sem[s], 1)
        done((s, tot[s], q), r, w)

    def dma(q, pairs, r=(), w=()):
        need(q, r, w)
        s = "dm%d" % ndma[0]
        ndma[0] += 1
        for o, i in pairs:
            QU[q].dma_start(o, i).then_inc(T.sem[s], 16)
        tot[s] = 16 * len(pairs)
        done((s, tot[s], "d" + s), r, w)

    def mm(out, pairs, r, w, first=True, last=True):
        need("t", r, w)
        for k, (l, x) in enumerate(pairs):
            ins = g.tensor.matmul(out, l, x, first and k == 0, last and k == len(pairs) - 1)
            if k == len(pairs) - 1:
                tot["qt"] = tot.get("qt", 0) + 1
                ins.then_inc(T.sem.qt, 1)
                done(("qt", tot["qt"], "t"), r, w)

    def ts(out, i, s1, o1, s2=None, o2=None, r=(), w=()):
        if o2 is None:
            op("v", lambda e: e.tensor_scalar(out, i, s1, None, o1), r, w)
        else:
            op("v", lambda e: e.tensor_scalar(out, i, s1, s2, o1, o2), r, w)

    def tt(out, a, b, o, r, w):
        op("v", lambda e: e.tensor_tensor(out, a, b, o), r, w)

    def cp(out, i, r, w, q="v"):
        if q == "v":
            op("v", lambda e: e.tensor_copy(out, i), r, w)
        else:
            op("s", lambda e: e.activation(out, i, AF.Identity), r, w)

    own = rank * 160
    nearH = 0 if topo.host(T.cores[0]) == topo.host(core) else 1
    partner = [c for c in T.cores if c != core and c in topo.cores_of(core)]
    near = [c for c in T.cores if topo.host(c) == topo.host(core) and c != core and c not in partner]
    far = [c for c in T.cores if topo.host(c) != topo.host(core)]
    far = [c for c in far if topo.same_plane(core, c)] + [c for c in far if not topo.same_plane(core, c)]
    offe = topo.engines(core, far[0])
    one = [e for e in topo.engines(core, partner[0]) if e not in offe]
    moff, mon = sum(1 << e for e in offe), sum(1 << e for e in one)

    def send(kind, e):
        name = "A%s%d" % (kind.upper(), e)
        src = T[name][:, own:own + 160]
        need("g", [name + "o"], [])

        def tr(dst, m, sem):
            ids = []
            for c in dst:
                rid, pid = topo.addr(c, core)
                ids.append(DstId(rid=rid, pnc=pid))
            return RemoteDMATransfer(dst_ids=ids, dma_engine_mask=m, remote_sem=T.sem[sem], srcs=[src],
                                     dsts=[src for _ in dst], alu_op=0)
        g.remote_dma_fused([tr(partner, mon, "r%sn%d" % (kind, e)), tr(near, moff, "r%sn%d" % (kind, e))], local_sem=T.sem.ls)
        g.remote_dma_fused([tr(far, moff, "r%sf%d" % (kind, e))], local_sem=T.sem.ls)
        tot["ls"] = tot.get("ls", 0) + len(one) + 2 * len(offe)
        for s, n in (("n", len(one) + len(near) * len(offe)), ("f", len(far) * len(offe))):
            sem = "r%s%s%d" % (kind, s, e)
            tot[sem] = n
            lastw[name + s] = [(sem, n, "x")]

    def wr(sd, G):
        o = 64 * sd + 32 * (G // 2)
        return slice(o + G % 2, o + 32, 2)

    for q, sd, t, k in (("y", 0, T.lw, "XA"), ("s", 1, T.rw, "XB")):
        dma(q, [(T.X[wr(sd, G), :, h, :], t[16 * (2 * G + h):16 * (2 * G + h) + 16, :])
                for G in range(4) for h in range(2)], [], [k])
    dma("y", [(T.RAW[:], T.opts[:])], [], ["RAW"])

    def iota(name, pat, base=0, ch=0):
        if name in ("CI", "mI", "slT"):
            out = T.CI[:, 0:1] if name == "CI" else T[name][:]
            op("g", lambda e: e.iota(out, pat, base, ch), [], [name])
        else:
            op("g", lambda e: e.iota(T[name][:], pat, base, ch, allow_small_or_imprecise_dtypes=True), [], [name])
    iota("CI", [[0, 1]], 0, 1)
    iota("ci", [[1, 143]])
    iota("kr", [[16, 2], [0, 4], [1, 16]])
    names = ["p", "i", "i8", "pg", "sd", "Gp", "xi", "xG", "rs", "g1", "gG", "b0", "b1", "b2", "xh", "Gh"]
    spec = [None, (0, 15), (0, 7), (4, 7), (6, 1), (4, 3), (1, 15), (0, 1), (3, 1), (4, 1), (5, 3), (0, 1), (1, 1), (2, 1),
            (5, 1), (5, 1)]
    for k, s in enumerate(spec):
        if s:
            ts(T.CI[:, k:k + 1], T.CI[:, 0:1], s[0], A.logical_shift_right, s[1], A.bitwise_and, ["CI"], ["CI%d" % k])
    cp(T.CF[:], T.CI[:], ["CI"] + ["CI%d" % k for k in range(1, 16)], ["CF"])
    col = {n: T.CF[:, k:k + 1] for k, n in enumerate(names)}
    ckey = {n: "CF" for n in names}
    nc = [0]

    def mk(name, src, s1, o1, s2=None, o2=None):
        def val(s):
            return col[s] if isinstance(s, str) else s
        k = nc[0]
        nc[0] += 1
        rk = [ckey[src]] + [ckey[s] for s in (s1, s2) if isinstance(s, str)]
        ts(T.CC[:, k:k + 1], col[src], val(s1), o1, val(s2), o2, rk, ["CC%d" % k])
        col[name], ckey[name] = T.CC[:, k:k + 1], "CC%d" % k

    def ma(name, src, m, a):
        mk(name, src, m, A.mult, a, A.add)
    ma("sgn", "sd", 2.0, -1.0)
    for b in range(2):
        aw = T["AW%d" % b]
        for c in range(5):
            ts(aw[:, own + c * 32:own + c * 32 + 32], T.X[:, b, :, c::5], col["sgn"], A.mult, None, None,
               ["XA", "XB", ckey["sgn"]], ["AW%do" % b])
        send("w", b)
    iota("mI", [[1, 82], [0, 16]])
    iota("slT", [[16, 10], [0, 8]])
    iota("RS", [[0, 10], [1, 8]])
    iota("bI", [[1, 256]])
    iota("KC", [[0, 10], [-16384, 8]], 141312)
    iota("pr", [[1, 8], [0, 16]])
    cp(T.nf[:], T.RAW[:], ["RAW"], ["nf"])
    ts(T.tf[:], T.nf[:], 0.2, A.mult, -0.4, A.add, ["nf"], ["tf"])
    cp(T.yi[:], T.tf[:], ["tf"], ["yi"])
    ts(T.C[:], T.nf[:], 10240.0, A.is_ge, 5120.0, A.mult, ["nf"], ["C"])

    def terms(acc, lst, n):
        st, kacc = [], "C"
        for j, (f, x, kx, sh) in enumerate(lst):
            s, t, ks, kt = T["si%d" % (j % 3)][:, 0:n], T["tf%d" % (j % 3)][:, 0:n], "si%d" % (j % 3), "tf%d" % (j % 3)
            one = [None, (ts, (t, x, float(f), A.mult, None, None, [kx], [kt])), (tt, (acc, acc, t, A.add, [kacc, kt], [kacc]))]
            if sh:
                one[0] = (ts, (s, x, sh, A.logical_shift_right, None, None, [kx], [ks]))
                one[1] = (ts, (t, s, float(f), A.mult, None, None, [ks], [kt]))
            st += [(2 * j + 3 * k, j, o) for k, o in enumerate(one) if o]
        return [o for _, _, o in sorted(st, key=lambda z: z[:2])]

    def run(steps):
        for f, a in steps:
            f(*a)
    run(terms(T.C[:], [(32, T.nf[:], "nf", 0), (-159, T.yi[:], "yi", 0)] +
              [(f, T.yi[:], "yi", sh) for sh, f in ((4, 5104), (5, -10224), (6, 608), (8, -2400), (10, 1920))], 160))
    cp(T.ti[:], T.C[:], ["C"], ["ti"])
    ts(T.hI[:], T.ti[:], 7, A.logical_shift_right, None, None, ["ti"], ["hI"])
    ts(T.lI[:], T.ti[:], 127, A.bitwise_and, None, None, ["ti"], ["lI"])
    for c in range(5):
        cp(T.HB[:, :, c, :], T.hI[:, c::5], ["hI"], ["HB%d" % c])
        cp(T.LB[:, :, c, :], T.lI[:, c::5], ["lI"], ["LB%d" % c])
    ma("a4", "gG", 16.0, "i8")
    ma("th", "rs", 64.0, "a4")
    mk("tlo", "th", 8.0, A.add)
    ma("m0", "g1", -1.0, 1.0)

    mats = {}

    def mat(name, buf, k, width, step, row, rk, t, wgt):
        ap = T[buf][:, k * step:k * step + width]
        rks = [rk, ckey[t]] + ([ckey[wgt]] if isinstance(wgt, str) else [])
        ts(ap, row, col[t], A.is_equal, col[wgt] if isinstance(wgt, str) else wgt, A.mult, rks, ["M" + name])
        mats[name] = (buf, k * step)

    def lz(name, a):
        buf, k = mats[name]
        return T[buf][:, k + 15 - a:k + 143 - a]

    def lm(name):
        buf, k = mats[name]
        return T[buf][:, k:k + 128]
    c128 = T.ci[:, 0:128]
    for k, (n, t, m) in enumerate((("TH0", "th", "m0"), ("TL0", "tlo", "m0"), ("TH1", "th", "g1"), ("TL1", "tlo", "g1"))):
        mat(n, "M8", k, 128, 128, c128, "ci", t, m)
    hb = ["HB%d" % c for c in range(5)] + ["LB%d" % c for c in range(5)]
    for b in range(2):
        for h in range(2):
            o = (b * 2 + h) * 80
            mm(T.P6[:, o:o + 80], [(lm("TH%d" % h), T.HB[:, b, :, :]), (lm("TL%d" % h), T.LB[:, b, :, :])],
               ["MTH%d" % h, "MTL%d" % h] + hb, ["P6"])
    for b in range(2):
        for h in range(2):
            o = (b * 2 + h) * 80
            cp(T.T4[:, b, :, h, :], T.P6[:, o:o + 80], ["P6"], ["T4%d%d" % (b, h)])
        cp(T["AO%d" % b][:, own:own + 160], T.T4[:, b, :, :, :], ["T4%d0" % b, "T4%d1" % b], ["AO%do" % b])
        send("o", b)
    ma("swr", "rs", -128.0, 64.0)
    ma("a3", "pg", 8.0, "i8")
    ma("qt", "rs", 64.0, "a3")
    mk("qst", "qt", "swr", A.add)
    ma("kc", "sd", 16.0, "i")
    ma("xq", "xh", 2.0, "xG")
    ma("kw", "sd", -16.0, 16.0)
    mk("kcw", "kw", "xi", A.add)
    for k in range(4):
        mk("mG%d" % k, "Gp", float(k), A.is_equal)
        mk("mX%d" % k, "xq", float(k), A.is_equal)
    mat("QN", "M4", 0, 128, 128, c128, "ci", "qt", 1.0)
    mat("QS", "M4", 1, 128, 128, c128, "ci", "qst", 1.0)
    mm(T.P5[:, 0:160], [(lm("QN"), T.C[:])], ["MQN", "C"], ["P5"])
    mm(T.P5[:, 160:320], [(lm("QS"), T.C[:])], ["MQS", "C"], ["P5"])
    cp(T.LQn[:], T.P5[:, 0:160], ["P5"], ["LQn"])
    cp(T.LQs[:], T.P5[:, 160:320], ["P5"], ["LQs"])
    ts(T.eQ[:], T.P5[:, 0:160], 10240.0, A.is_ge, None, None, ["P5"], ["eQ0"])
    lastw["eQ1"] = lastw["eQ0"]
    for k in range(4):
        mat("WG%d" % k, "M4", 7 + k, 128, 128, T.kr[:], "kr", "kcw", "mX%d" % k)
        mat("RG%d" % k, "M8", 4 + k, 128, 128, T.kr[:], "kr", "kc", "mG%d" % k)

    turn = [0]

    def through(e, H, out, okey, tile, tkeys, m, eng, Gs=(0, 1, 2, 3)):
        for G in Gs:
            for k in range(2):
                pk = "P%d" % (turn[0] % 4)
                o = (e % 2) * 5120 + H * 2560 + G * 640 + k * 320
                mm(T[pk][:, 0:320], [(lm("%s%d" % (m, G)), tile[:, H * 640 + k * 320:H * 640 + k * 320 + 320])],
                   ["M%s%d" % (m, G)] + tkeys, [pk])
                cp(out[:, o:o + 320], T[pk][:, 0:320], [pk], ["%s%d" % (okey, o)], eng[turn[0] % 2])
                turn[0] += 1

    def slots_in(e, eng):
        for H in (nearH, 1 - nearH):
            through(e, H, T.OT, "OT", T["AO%d" % e], ["AO%do" % e, "AO%dn" % e] if H == nearH else ["AO%df" % e], "RG", eng)

    def walls_pe(e, eng):
        through(e, nearH, T.W, "W", T["AW%d" % e], ["AW%do" % e, "AW%dn" % e], "WG", eng, (0, 1))

    def walls_dma(e, H, halves):
        aw = T["AW%d" % e]
        for u in halves:
            c0 = (e % 2) * 5120 + H * 2560 + u * 1280
            dma("y", [(T.W[16 * q:16 * q + 16, c0:c0 + 1280],
                       aw[(64 if q < 4 else 0) + 32 * u:(96 if q < 4 else 32) + 32 * u, H * 640:H * 640 + 640])
                      for q in range(8)], ["AW%do" % e, "AW%dn" % e] if H == nearH else ["AW%df" % e],
                ["W%d" % (c0 + 320 * k) for k in range(4)])
    for e in range(2):
        walls_dma(e, nearH, (1,))
        walls_dma(e, 1 - nearH, (0, 1))
    walls_pe(0, "ss")
    walls_pe(1, "ss")
    slots_in(0, "ss")
    mk("lo", "i", 8.0, A.is_ge)
    ma("w", "lo", -127.0, 128.0)
    ma("wn", "lo", -1.0, 1.0)
    mk("hbw", "wn", -BIG, A.mult)
    mk("e80", "wn", 80.0, A.mult)
    ma("sw", "sd", -128.0, 64.0)
    ma("tz", "pg", 16.0, 15.0)
    mk("tzs", "tz", "sw", A.add)
    ma("tl0", "pg", 16.0, "i8")
    mk("tl1", "tl0", 8.0, A.add)
    mk("tl0s", "tl0", "sw", A.add)
    mk("tl1s", "tl1", "sw", A.add)
    ma("a0", "i", 2.0, "g1")
    ma("a1", "Gh", 32.0, "a0")
    ma("tp", "sd", 64.0, "a1")
    mk("tps", "tp", "sw", A.add)
    ma("a2", "xq", 16.0, "xi")
    ma("xst", "sd", 64.0, "a2")
    mk("xot", "xst", "sw", A.add)
    mk("tm", "i", 1024.0, A.mult)
    mk("w1", "b2", "w", A.mult)
    mk("w0", "w", "w1", A.subtract)
    ma("t2", "b2", -4.0, "i8")
    ma("t3", "pg", 16.0, "t2")
    ma("a5", "sd", -0.5, 0.25)
    mk("tb", "tm", "a5", A.add)
    ma("a6", "b1", 3.0, 1.0)
    ma("a7", "b2", 15.0, 1.0)
    ma("a8", "b0", 1.0 / 128, 1.0 / 128)
    mk("a9", "a8", "a6", A.mult)
    mk("c1", "a9", "a7", A.mult)
    ma("s8", "i8", -1.0, 8.0)
    op("v", lambda e: e.memset(T.W[:, E:E + 8], -BIG), [], ["We"])
    op("v", lambda e: e.memset(T.OT[:, E:E + 16], 0.0), [], ["OTz"])
    cp(T.OT[:, E:E + 1], col["e80"], [ckey["e80"], "OTz"], ["OTe"])
    ts(T.slU[:], T.slT[:], col["i"], A.add, None, None, ["slT", "CF"], ["slU"])
    mat("XO", "M4", 2, 128, 128, c128, "ci", "xot", 1.0)
    mat("XS", "M4", 3, 128, 128, c128, "ci", "xst", -1.0)

    def own_walls(b, src, ksrc):
        mm(T.P7[:, 0:160], [(lm("XO"), src)], ["MXO", ksrc], ["P7"])
        mm(T.P7[:, 160:320], [(lm("XS"), src)], ["MXS", ksrc], ["P7"])
        cp(T["XO%d" % b][:], T.P7[:, 0:160], ["P7"], ["XO%d" % b])
        ts(T["xs%d" % b][:], T.P7[:, 160:320], col["tm"], A.add, None, None, ["P7", ckey["tm"]], ["xs%d" % b])
        cp(T["x%d" % b][:], T["XO%d" % b][:].indirect(T.slU[:]), ["XO%d" % b, "slU"], ["x%d" % b], "s")
    zk = (("ZKs", "tzs", "w"), ("ZK", "tz", "w"), ("Z1", "tz", 1.0), ("ZV", "tz", -262144.0), ("ZVs", "tzs", -262144.0))
    for k, (n, t, m) in enumerate(zk):
        mat(n, "MZ", k, 143, 144, T.ci[:], "ci", t, m)
    ts(T.DL[:], T.ci[:, 0:16], col["i"], A.is_equal, None, None, ["ci", "CF"], ["DL"])
    ts(T.mI[:], T.mI[:], 7, A.bitwise_and, None, None, ["mI"], ["mI"])
    ts(T.MB[:], T.mI[:], col["i8"], A.is_equal, None, None, ["mI", "CF"], ["MB"])
    ts(T.RS[:], T.RS[:], 0.5, A.is_gt, None, None, ["RS"], ["RS"])
    ts(T.H2[:], T.RS[:], 2.0, A.mult, None, None, ["RS"], ["H2"])

    def empties(eq, keq):
        for k in range(16):
            op("s", lambda e: e.activation(T.EX[:, :, k], eq, AF.Identity, scale=T.DL[:, k:k + 1]), [keq, "DL"], ["EX%d" % k])
        mm(T.P5[:, 0:80], [(lz("Z1", a), T.EX[:, 5 * a:5 * a + 5, :]) for a in range(16)],
           ["MZ1"] + ["EX%d" % k for k in range(16)], ["P5"])
    for dst, sc in (("f1", 1.0), ("f2", 0.5)):
        ts(T[dst][:], T.bI[:], col["c1"], A.mult, sc, A.mult, ["bI", ckey["c1"]], [dst])
        ts(T[dst][:], T[dst][:], -0.5 + 2.0 ** -9, A.add, None, None, [dst], [dst])
        ts(T[dst][:], T[dst][:], MG, A.add, MG, A.subtract, [dst], [dst])
    ts(T.f2[:], T.f2[:], -2.0, A.mult, None, None, ["f2"], ["f2"])
    tt(T.f1[:], T.f1[:], T.f2[:], A.add, ["f1", "f2"], ["f1"])
    ts(T.F9[:], T.ci[:, 0:9], col["s8"], A.is_equal, None, None, ["ci", ckey["s8"]], ["F9"])
    for k in range(9):
        ts(T.F[:, k::9], T.f1[:], T.F9[:, k:k + 1], A.max, None, None, ["f1", "F9"], ["F%d" % k])
    kF = ["F%d" % k for k in range(9)]
    for k, (n, t) in enumerate((("LQ0", "tl0"), ("LQ1", "tl1"), ("LQ0s", "tl0s"), ("LQ1s", "tl1s"))):
        mat(n, "M8", 8 + k, 128, 128, c128, "ci", t, "w")
    for h in range(2):
        for n in range(2):
            mk("tn%d%d" % (h, n), "t3", 8.0 * h + 4.0 * n, A.add)
            for k in range(2):
                mat("LN%d%d%d" % (h, n, k), "M8", 13 + 4 * h + 2 * n + k, 128, 128, c128, "ci", "tn%d%d" % (h, n), "w%d" % k)
    mat("HA", "M8", 12, 128, 128, T.pr[:], "pr", "pg", "hbw")
    mat("P1", "M4", 4, 128, 128, c128, "ci", "tp", 1.0)
    mat("P2", "M4", 5, 128, 128, c128, "ci", "tp", 0.5)
    mat("P3", "M4", 6, 128, 128, c128, "ci", "tps", -0.5)
    tt(lm("P2"), lm("P2"), lm("P3"), A.add, ["MP2", "MP3"], ["MP2"])

    kW = ["We"] + ["W%d" % (320 * k) for k in range(32)]
    kOT = ["OTe"] + ["OT%d" % (320 * k) for k in range(32)]
    W, OT = T.W[:, 0:E + 8], T.OT[:, 0:E + 16]

    def invert(b):
        f, i, v = T.nf[:, 0:80], T.ti[:, 0:80], T.hI[:, 0:80]
        acc, y = T.C[:, 0:80], T.yi[:, 0:80]
        a = [(cp, (i, T.QF[:], ["QF"], ["ti"])), (ts, (acc, T.QF[:], 10240.0, A.is_ge, 10080.0, A.mult, ["QF"], ["C"])),
             (ts, (v, i, 5, A.logical_shift_right, None, None, ["ti"], ["hI"])),
             (ts, (f, v, 0.2, A.mult, -0.4, A.add, ["hI"], ["nf"])), (cp, (y, f, ["nf"], ["yi"]))]
        a += terms(acc, [(5, T.QF[:], "QF", 0), (80, i, "ti", 4), (-319, i, "ti", 5), (1275, y, "yi", 0)] +
                   [(k, y, "yi", sh) for sh, k in ((2, -4800), (4, 3840), (5, -10160))], 80)
        return a + [(cp, (T.YO[:, b * 80 + c:b * 80 + 80:5], T.C[:, c * 16:c * 16 + 16], ["C"], ["YO%d" % b])) for c in range(5)]

    def put_slots(b):
        dma("y", [(T.yo[16 * gg + 8 * sd:16 * gg + 8 * sd + 8, b * 80:b * 80 + 80],
                   T.YO[64 * sd + 8 * gg:64 * sd + 8 * gg + 8, b * 80:b * 80 + 80]) for sd in range(2) for gg in range(8)],
            ["YO%d" % b], [])

    def turn_walls(b, src, ks):
        for c in range(5):
            ts(T.Y[:, b, :, c::5], src[:, c * 32:c * 32 + 32], col["sgn"], A.mult, None, None, [ks, ckey["sgn"]], ["Y%d" % b])

    def put_walls(b, qs):
        for sd, o in ((0, T.yl), (1, T.yr)):
            dma(qs[sd], [(o[16 * (2 * G + h):16 * (2 * G + h) + 16, b * 80:b * 80 + 80], T.Y[wr(sd, G), b, h, :])
                         for G in range(4) for h in range(2)], ["Y%d" % b], [])

    def rnd(t):
        b = t % 2
        e = t + 2
        lqn = (T.LQn[:, b * 80:b * 80 + 80], T.LQs[:, b * 80:b * 80 + 80]) if t < 2 else (T.LMn[:], T.LMs[:])
        kl = ("LQn", "LQs") if t < 2 else ("LMn", "LMs")
        x, kx = T["x%d" % b][:], "x%d" % b
        empties(T.eQ[:, 80 * b:80 * b + 80], "eQ%d" % b)
        op("s", lambda q: q.activation(T.u[:], W.indirect(lqn[0]), AF.Identity), kW + [kl[0]], ["u"])
        op("v", lambda q: q.tensor_tensor(T.gO[:], OT.indirect(lqn[1]), T.MB[:, 16 * t:16 * t + 1280], A.mult), kOT + [kl[1], "MB"], ["gO"])
        mm(T.P0[:, 0:80], [(lz("ZKs", a), T.gO[:, 80 * a:80 * a + 80]) for a in range(16)], ["MZKs", "gO"], ["P0"])
        mm(T.P1[:, 0:80], [(lz("ZK", a), T.gO[:, 80 * a:80 * a + 80]) for a in range(16)], ["MZK", "gO"], ["P1"])

        ms = [1 + (t + 3 * q) % 7 for q in range(2)]

        def diffs(q):
            m, d = ms[q], T["d%d" % q]
            hb = m.bit_length() - 1
            need("v", ["u"], ["d%d" % q])
            for k in range(1 << hb):
                out = d[:] if hb == 0 else d[:, :, :, k] if hb == 1 else d[:, :, k >> 1, k & 1]
                tt(out, T.u[:, (k ^ m)::2 << hb], T.u[:, k::2 << hb], A.subtract, ["u"], ["d%d_%d" % (q, k)])
            done(("qv", tot["qv"], "v"), [], ["d%d" % q])

        def parts(q):
            m, d, vv = ms[q], T["d%d" % q], T["V%d" % q]
            hb = m.bit_length() - 1
            f = m ^ (1 << hb)
            need("s", ["d%d" % q], ["V%d" % q])

            def act(o, i, s):
                op("s", lambda qq: qq.activation(o, i, AF.Relu, scale=s), ["d%d" % q], [])
            if hb == 0:
                act(vv[:, :, :, :, 0], d[:], -1.0)
                act(vv[:, :, :, :, 1], d[:], 1.0)
            elif hb == 1:
                act(vv[:, :, :, 0, :], d[:], -1.0)
                if f == 0:
                    act(vv[:, :, :, 1, :], d[:], 1.0)
                else:
                    for k in range(2):
                        act(vv[:, :, :, 1, 1 - k], d[:, :, :, k], 1.0)
            else:
                act(vv[:, :, 0, :, :], d[:], -1.0)
                if f == 0:
                    act(vv[:, :, 1, :, :], d[:], 1.0)
                for k in range(2 if f else 0):
                    if f == 1:
                        act(vv[:, :, 1, :, 1 - k], d[:, :, :, k], 1.0)
                    else:
                        act(vv[:, :, 1, 1 - k, :], d[:, :, k, :], 1.0)
            done(("qs", tot["qs"], "s"), [], ["V%d" % q])

        def sums(q):
            mm(T["P%d" % (2 + q)][:, 0:80], [(lz("Z1", a), T["V%d" % q][:, 10 * a:10 * a + 10, :, :, :]) for a in range(16)],
               ["MZ1", "V%d" % q], ["P%d" % (2 + q)])

        def gone():
            for q in range(2):
                ts(T["g%d" % q][:], T["P%d" % (2 + q)][:, 0:80], 0.5, A.is_lt, None, None, ["P%d" % (2 + q)], ["g%d" % q])
            for q in range(2):
                gt, gk, m = T["g%d" % q], "g%d" % q, ms[q]
                st = 2 << (m.bit_length() - 1)
                need("v", [gk], [])
                for k in range(st // 2):
                    op("v", lambda qq: qq.tensor_tensor(gt[:, k::st], gt[:, k::st], gt[:, (k ^ m)::st], A.is_gt))
                done(("qv", tot["qv"], "v"), [], [gk])
        cp(T.L1[:], T.P0[:, 0:80], ["P0"], ["L1"])
        cp(T.L2[:], T.P1[:, 0:80], ["P1"], ["L2"])
        op("v", lambda q: q.tensor_tensor(T.cm1[:], W.indirect(T.L1[:]), x, A.is_gt), kW + ["L1", kx], ["cm1"])
        mm(T.P4[:, 0:80], [(lz("ZV", a), T.cm1[:, a::16]) for a in range(16)], ["MZV", "cm1"], ["P4"], True, False)
        for q in range(2):
            diffs(q)
            parts(q)
            sums(q)
        op("v", lambda q: q.tensor_tensor(T.cm2[:], W.indirect(T.L2[:]), x, A.is_lt), kW + ["L2", kx], ["cm2"])
        mm(T.P4[:, 0:80], [(lz("ZVs", a), T.cm2[:, a::16]) for a in range(16)], ["MZVs", "cm2"], ["P4"], False, True)
        tt(T.kb[:], T.KC[:], T.P0[:, 0:80], A.subtract, ["KC", "P0"], ["kb"])
        gone()
        tt(T.gs[:], T.g0[:], T.g1[:], A.max, ["g0", "g1"], ["gs"])
        ts(T.gm[:], T.gs[:], -262144.0, A.mult, None, None, ["gs"], ["gm"])
        tt(T.gb[:], T.P5[:, 0:80], T.gs[:], A.max, ["gs", "P5"], ["gb"])
        tt(T.kb2[:], T.kb[:], T.gm[:], A.add, ["kb", "gm"], ["kb2"])
        op("v", lambda q: q.tensor_tensor_scan(T.sc[:], T.H2[:], T.gb[:], 0.0, A.mult, A.add), ["H2", "gb"], ["sc"])
        tt(T.da[:], T.P4[:, 0:80], T.kb2[:], A.add, ["P4", "kb2"], ["da"])
        ts(T.fb[:], T.sc[:, 7::8], 9.0, A.mult, None, None, ["sc"], ["fb"])
        op("v", lambda q: q.tensor_tensor_scan(T.RM[:], T.RS[:], T.da[:], 0.0, A.mult, A.max), ["RS", "da"], ["RM"])
        cp(T.Mi[:], T.RM[:, 7::8], ["RM"], ["Mi"])
        ts(T.cd[:], T.Mi[:], 14, A.logical_shift_right, None, None, ["Mi"], ["cd"])
        ts(T.cv[:], T.Mi[:], 16383, A.bitwise_and, None, None, ["Mi"], ["cv"])
        tt(T.cx[:], T.cd[:], T.fb[:], A.add, ["cd", "fb"], ["cx"])
        ts(T.cu[:], T.cv[:], -1.0, A.mult, 10240.0, A.add, ["cv"], ["cu"])
        cp(T.iu[:], T.cx[:], ["cx"], ["iu"])
        op("s", lambda q: q.activation(T.FT[:], T.F[:].indirect(T.iu[:]), AF.Identity), kF + ["iu"], ["FT"])
        old, ko = T["AO%d" % t][:, own:own + 160], "AO%do" % t
        op("v", lambda q: q.tensor_tensor(T.dT[:], OT.indirect(T.cu[:]), old, A.subtract), kOT + ["cu", ko], ["dT"])
        tt(T.mT[:], T.dT[:], T.FT[:], A.mult, ["dT", "FT"], ["mT"])
        tt(T.TN[:], T.mT[:], old, A.add, ["mT", ko], ["TN"])
        for k in range(2):
            mm(T.P5[:, 40 * k:40 * k + 40], [(lm("LN%d%d%d" % (h, n, k)), T.TN[:, :, h, n::2]) for h in range(2) for n in range(2)],
               ["MLN%d%d%d" % (h, n, k) for h in range(2) for n in range(2)] + ["TN"], ["P5"])
        cp(T.LN[:], T.P5[:, 0:80], ["P5"], ["LN"])
        if t < 2:
            cp(T["AO%d" % e][:, own:own + 160], T.TN[:], ["TN"], ["AO%do" % e], "s")
            send("o", e)
        mm(T.P4[:, 160:240], [(lm("LQ0"), T.TN[:, :, 0, :]), (lm("LQ1"), T.TN[:, :, 1, :])], ["MLQ0", "MLQ1", "TN"], ["P4"])
        for k in range(2):
            cp(T.w[:, 320 * k:320 * k + 320], W.indirect(T.LN[:, 20 * k:20 * k + 20]), kW + ["LN"], ["w%d" % k], "s")
        inv = []
        if t > 0:
            cp(T.QF[:], T.P4[:, 160:240], ["P4"], ["QF"])
            inv = invert(b) if t == 2 else []
        ts(T.nd[:], T.TN[:], 79.5, A.is_lt, None, None, ["TN"], ["nd"])
        run(inv[0:5])
        mm(T.P6[:, 0:160], [(lm("HA"), T.nd[:])], ["MHA", "nd"], ["P6"])
        for k in range(2):
            o = 320 * k
            op("v", lambda q: q.tensor_tensor(T.t1[:, o:o + 320], W.indirect(T.LN[:, 40 + 20 * k:60 + 20 * k]), T.w[:, o:o + 320], A.max),
               kW + ["LN", "w%d" % k], ["t1%d" % k])
        tt(T.xx[:], T.P6[:, 0:160], T["xs%d" % b][:], A.add, ["P6", "xs%d" % b], ["xx"])
        tt(T.t2[:], T.t1[:, 0::2], T.t1[:, 1::2], A.max, ["t10", "t11"], ["t2"])
        for h in range(2):
            for n in range(2):
                tt(T.m4[:, :, h, n::2], T.t2[:, :, :, h, n, 0], T.t2[:, :, :, h, n, 1], A.max, ["t2"], ["m4%d%d" % (h, n)])
        tt(T.mm[:], T.m4[:], T.xx[:], A.max, ["m400", "m401", "m410", "m411", "xx"], ["mm"])
        ts(T.nn[:], T.mm[:], -1.0, A.mult, col["tb"], A.add, ["mm", ckey["tb"]], ["nn"])
        mm(T.P6[:, 0:160], [(lm("P1"), T.nn[:])], ["MP1", "nn"], ["P6"])
        mm(T.P7[:, 0:160], [(lm("P2"), T.nn[:])], ["MP2", "nn"], ["P7"])
        run(inv[5:13])
        cp(T.pp[:], T.P6[:, 0:160], ["P6"], ["pp"], "s")
        tt(T.qq[:], T.P7[:, 0:160], T.pp[:], A.min, ["P7", "pp"], ["qq"])
        dst, kd = (T["AW%d" % e][:, own:own + 160], "AW%do" % e) if t < 2 else (T.RF[:], "RF")
        ts(dst, T.qq[:], MG, A.add, MG, A.subtract, ["qq"], [kd])
        if t < 2:
            send("w", e)
        return dst, kd, inv[13:]

    own_walls(0, T.AW0[:, own:own + 160], "AW0o")
    slots_in(1, "sv")
    dst, kd, inv = rnd(0)
    own_walls(1, T.AW1[:, own:own + 160], "AW1o")
    mm(T.P4[:, 240:320], [(lm("LQ0s"), T.TN[:, :, 0, :]), (lm("LQ1s"), T.TN[:, :, 1, :])], ["MLQ0s", "MLQ1s", "TN"], ["P4"])
    for c in range(5):
        cp(T.LMn[:, c::5], T.P4[:, 160 + c * 16:176 + c * 16], ["P4"], ["LMn"])
        cp(T.LMs[:, c::5], T.P4[:, 240 + c * 16:256 + c * 16], ["P4"], ["LMs"])
    ts(T.eQ[:, 0:80], T.LMn[:], 10240.0, A.is_ge, None, None, ["LMn"], ["eQ0"])
    own_walls(0, dst, kd)
    for H in (nearH, 1 - nearH):
        walls_dma(2, H, (0, 1))
    slots_in(2, "sv")
    dst, kd, inv = rnd(1)
    turn_walls(1, dst, kd)
    run(invert(1))
    for H in (nearH, 1 - nearH):
        walls_dma(3, H, (0, 1))
    slots_in(3, "sv")
    put_walls(1, "yy")
    put_slots(1)
    dst, kd, inv = rnd(2)
    turn_walls(0, dst, kd)
    put_walls(0, "ys")
    run(inv)
    put_slots(0)
    for s in tot:
        if waited["g"].get(s, 0) < tot[s]:
            g.wait_ge(T.sem[s], tot[s])
